import numpy as np
import ml_dtypes


def mxq(x, axis, fmt="e4m3"):
    dtype, down = {"e4m3": (ml_dtypes.float8_e4m3fn, 7), "e5m2": (ml_dtypes.float8_e5m2, 14)}[fmt]
    v = np.moveaxis(np.asarray(x, np.float32).astype(ml_dtypes.bfloat16).astype(np.float64), axis, -1)
    blocks = v.reshape(v.shape[:-1] + (-1, 32))
    amax = np.abs(blocks).max(-1, keepdims=True)
    byte = np.maximum(np.where(amax > 0, np.frexp(amax)[1] - 1 + 127, 0) - down, 1)
    scale = np.exp2(byte - 127.0)
    codes = (blocks / scale).astype(np.float32).astype(dtype).astype(np.float64)
    return np.moveaxis((codes * scale).reshape(v.shape), -1, axis)


WIDE = False


def mx_kscale(k):
    if not WIDE:
        return np.ones(k)
    levels = np.array([18, -18])
    if k % 512:
        return np.exp2(np.random.permutation(np.resize(levels, k // 32))).repeat(32)
    a = np.empty((k // 512, 16))
    for p in range(k // 512):
        a[p, :8] = np.random.permutation(np.resize(levels, 8))
        for g in range(8):
            far = levels[np.abs(levels - a[p, g]) >= 10]
            a[p, g + 8] = far[np.random.randint(len(far))]
    return np.exp2(a.ravel()).repeat(32)


def f64(x):
    return np.asarray(x).astype(np.float64)


def striped(idx):
    return np.tile(np.asarray(idx).reshape(-1, 16).T, (8, 1)).astype(np.uint16)


def unstriped(offs):
    return offs[:16].T.reshape(-1).astype(np.int64)


E2M1 = np.array([0.0, 0.5, 1.0, 1.5, 2.0, 3.0, 4.0, 6.0, -0.0, -0.5, -1.0, -1.5, -2.0, -3.0, -4.0, -6.0])


def pack_weight(w, fmt):
    k, n = w.shape
    w = f64(np.asarray(w, np.float32).astype(ml_dtypes.bfloat16)).reshape(k // 32, 32, n)
    amax = np.abs(w).max(1)
    if fmt == "e4m3":
        byte = np.frexp(amax)[1] - 1 + 127 - 7
    else:
        mant, ex = np.frexp(amax / 6.0)
        byte = np.where(mant > 0.5, ex, ex - 1) + 127
    byte = np.clip(np.where(amax > 0, byte, 1), 1, 254)
    scaled = (w * np.exp2(127.0 - byte)[:, None, :]).reshape(k, n).astype(np.float32)
    by_word = np.ascontiguousarray(scaled.reshape(k // 512, 128, 4, n).transpose(0, 1, 3, 2))
    if fmt == "e4m3":
        words = by_word.astype(ml_dtypes.float8_e4m3fn).view(np.uint8)
    else:
        c = by_word.astype(ml_dtypes.float4_e2m1fn).view(np.uint8) & 0xF
        words = (c[..., 0::2] | (c[..., 1::2] << 4)).reshape(k // 512, 128, 2 * n)
    return np.ascontiguousarray(words), np.ascontiguousarray(byte.astype(np.uint8).reshape(k // 512, 16, n))


def unpack_weight(words, scales, fmt):
    g, _, n = scales.shape
    words = np.ascontiguousarray(words).reshape(g, 128, n, -1)
    if fmt == "e4m3":
        vals = words.view(ml_dtypes.float8_e4m3fn).astype(np.float64)
    else:
        nib = np.empty((g, 128, n, 4), np.uint8)
        nib[..., 0::2] = words & 0xF
        nib[..., 1::2] = words >> 4
        vals = E2M1[nib]
    vals = vals * np.repeat(np.exp2(scales.astype(np.float64) - 127.0), 8, axis=1)[..., None]
    return vals.transpose(0, 1, 3, 2).reshape(g * 512, n)


B, N, T, D, R = 1, 512, 2048, 512, 1024


def setup_inputs():
    n = np.random.standard_normal
    idx = np.random.permutation(T)[:B * N]
    s = mx_kscale(D)[:, None]
    z = mx_kscale(R)[:, None]
    x = n((B, D, R))
    wp = pack_weight(n((D, T)) * (1.00 / np.sqrt(D)) / s, "e4m3")
    return {
        "xT": (x * s).astype(np.float32),
        "w_words": wp[0],
        "w_scales": wp[1],
        "y": np.random.randint(0, 2, (B, R, N)).astype(np.float32),
        "wt": (np.random.uniform(0.5, 1.5, (B, R, 1)) * 1.0 / np.sqrt(R) * z).astype(np.float32),
        "xm": (x.transpose(0, 2, 1) / z).astype(np.float32),
        "offs": striped(idx),
    }


def reference(xT, w_words, w_scales, y, wt, xm, offs):
    idx = unstriped(offs)
    w = unpack_weight(w_words, w_scales, "e4m3")
    pick = lambda x: x[:, idx].reshape(x.shape[0], B, N).transpose(1, 0, 2)
    a = mxq(f64(xT), 1, "e4m3").transpose(0, 2, 1) @ pick(w)
    g = f64(wt) * (1.0 / (1.0 + np.exp(-a)) - f64(y))
    dw = mxq(f64(xm), 1, "e4m3").transpose(0, 2, 1) @ mxq(g, 1, "e5m2")
    gw = np.zeros((D, T))
    gw[:, idx] = dw.transpose(1, 0, 2).reshape(D, B * N)
    return gw

@@ -1,0 +1,209 @@
+from contextlib import ExitStack
+
+import concourse.mybir as mybir
+
+N, T, D, R = 512, 2048, 512, 1024
+FLOPS = 2 * 2 * R * N * D
+
+F32 = mybir.dt.float32
+BF16 = mybir.dt.bfloat16
+I32 = mybir.dt.int32
+U32 = mybir.dt.uint32
+U16 = mybir.dt.uint16
+U8 = mybir.dt.uint8
+E4 = mybir.dt.float8_e4m3fn_x4
+E5 = mybir.dt.float8_e5m2_x4
+ACT = mybir.ActivationFunctionType
+ALU = mybir.AluOpType
+
+P = 128
+PACK = 4
+KP = P * PACK
+PASSES = R // KP
+DBLOCKS = D // P
+WINDOWS = 3
+XT_V = (80, 64)
+
+
+def tile_attend_gnce_w_kernel(tc, xT, w_words, w_scales, y, wt, xm, offs, out):
+    nc = tc.nc
+    with ExitStack() as ctx:
+        keep = ctx.enter_context(tc.tile_pool(name="keep", bufs=1))
+        psum = ctx.enter_context(tc.psum_pool(name="psum", bufs=4))
+
+        def sb(name, shape, dtype):
+            return keep.tile(shape, dtype, name=name, align_bytes=64)
+
+        offsets = keep.tile([P, N // 16], U16, name="offsets")
+        nc.sync.dma_start(offsets[:], offs)
+
+        xt_raw = [sb("xt_raw%d" % c, [P, PACK, KP], F32) for c in range(PASSES)]
+        y_raw = [[sb("y_raw%d%d" % (c, h), [P, 2, N], F32) for h in range(2)] for c in range(PASSES)]
+        xm_raw = [[sb("xm_raw%d%d" % (c, h), [P, PACK, D // 2], F32) for h in range(2)] for c in range(PASSES)]
+        words = sb("words", [P, T], U32)
+        scales = sb("scales", [P, T], U8)
+        w_rows = sb("w_rows", [P, PASSES, PACK], F32)
+
+        def load_xt(c):
+            nc.sync.dma_start(out=xt_raw[c][:], in_=xT[0][:, c * KP:(c + 1) * KP].rearrange("(p j) r -> p j r", j=PACK))
+
+        def load_y(c):
+            rows = y[0][c * KP:(c + 1) * KP, :].rearrange("(p t) i -> p t i", t=PACK)
+            for h in range(2):
+                nc.sync.dma_start(out=y_raw[c][h][:], in_=rows[:, 2 * h:2 * h + 2, :])
+
+        def load_xm(h):
+            for c in range(PASSES):
+                rows = xm[0][c * KP:(c + 1) * KP, :].rearrange("(p t) d -> p t d", t=PACK)
+                nc.sync.dma_start(out=xm_raw[c][h][:], in_=rows[:, :, h * (D // 2):(h + 1) * (D // 2)])
+
+        load_xt(0)
+        nc.vector.memset(scales[:].bitcast(I32), 0)
+        for q in range(4):
+            nc.scalar.dma_start(out=scales[32 * q:32 * q + 4, :].bitcast(I32),
+                                in_=w_scales[0][4 * q:4 * q + 4, :].bitcast(I32))
+        nc.scalar.dma_start(out=w_rows[:], in_=wt[0].rearrange("(c p t) o -> p c (t o)", p=P, t=PACK))
+        nc.sync.dma_start(out=words[:].bitcast(I32), in_=w_words[0].rearrange("p n t -> p (n t)").bitcast(I32))
+        load_y(0)
+        load_xt(1)
+        load_y(1)
+        load_xm(0)
+        load_xm(1)
+
+        warm = sb("warm", [P, 16], F32)
+        nc.gpsimd.memset(warm[:], 0.0)
+        nc.scalar.activation(out=warm[:, 8:9], in_=warm[:, 0:1], func=ACT.Sigmoid)
+
+        windows = [sb("window%d" % k, [P, T], F32) for k in range(WINDOWS)]
+
+        w_scale_g = sb("w_scale_g", [P, N], U8)
+        w_word_g = sb("w_word_g", [P, N], U32)
+        nc.vector.tensor_copy(w_scale_g[:], scales[:].indirect(offsets[:]))
+
+        xt_codes = [sb("xt_codes%d" % c, [P, KP], U32) for c in range(PASSES)]
+        xt_scale = [sb("xt_scale%d" % c, [P, KP], U8) for c in range(PASSES)]
+        g_codes = [sb("g_codes%d" % c, [P, N], U32) for c in range(PASSES)]
+        g_scale = [sb("g_scale%d" % c, [P, N], U8) for c in range(PASSES)]
+        sig = [[None] * PACK for c in range(PASSES)]
+        wy = [[None] * PACK for c in range(PASSES)]
+        g_rows = [sb("g_rows%d" % c, [P, PACK, N], BF16) for c in range(PASSES)]
+        g_packed = [sb("g_packed%d" % c, [P, N, PACK], BF16) for c in range(PASSES)]
+
+        def quant_xt(c):
+            xb = sb("xt_bf%d" % c, [P, PACK, P, PACK], BF16)
+            dst = xb[:].rearrange("p t m j -> p m j t")
+            srcv = xt_raw[c][:].rearrange("p j (m t) -> p m j t", t=PACK)
+            mv = XT_V[c]
+            nc.vector.tensor_copy(out=dst[:, :mv], in_=srcv[:, :mv])
+            nc.scalar.copy(out=dst[:, mv:], in_=srcv[:, mv:])
+            nc.vector.quantize_mx(out=xt_codes[c][:].bitcast(E4), scales=xt_scale[c][:],
+                                  in_=xb[:].rearrange("p t m j -> p (t m j)"))
+
+        def scores(c, t):
+            acc = psum.tile([P, N], F32, name="acc_a", tag="acc_a")
+            cols = slice(t * P, (t + 1) * P)
+            nc.tensor.matmul_mx(out=acc[:], lhsT=xt_codes[c][:, cols].bitcast(E4), lhsT_scale=xt_scale[c][:, cols],
+                                rhs=w_word_g[:].bitcast(E4), rhs_scale=w_scale_g[:], start=True, stop=True)
+            sig[c][t] = sb("sig%d%d" % (c, t), [P, N], F32)
+            nc.scalar.activation(out=sig[c][t][:], in_=acc[:], func=ACT.Sigmoid)
+
+        def weigh_y(c, t, on_vector):
+            wy[c][t] = sb("wy%d%d" % (c, t), [P, N], F32)
+            src = y_raw[c][t // 2][:, t % 2, :]
+            if on_vector:
+                nc.vector.tensor_scalar_mul(wy[c][t][:], src, w_rows[:, c, t:t + 1])
+            else:
+                nc.scalar.activation(out=wy[c][t][:], in_=src, func=ACT.Copy, scale=w_rows[:, c, t:t + 1])
+
+        def grad(c, t, cols):
+            nc.vector.scalar_tensor_tensor(out=g_rows[c][:, t, cols], in0=sig[c][t][:, cols], scalar=w_rows[:, c, t:t + 1],
+                                           in1=wy[c][t][:, cols], op0=ALU.mult, op1=ALU.subtract)
+
+        def pack_g(c, cols, on_vector):
+            dst = g_packed[c][:, cols, :].rearrange("p (q i) t -> p q t i", i=4)
+            srcv = g_rows[c][:, :, cols].rearrange("p t (q i) -> p q t i", i=4)
+            if on_vector:
+                nc.vector.tensor_copy(out=dst, in_=srcv)
+            else:
+                nc.scalar.copy(out=dst, in_=srcv)
+
+        def quant_g(c, cols):
+            nc.vector.quantize_mx(out=g_codes[c][:, cols].bitcast(E5), scales=g_scale[c][:, cols],
+                                  in_=g_packed[c][:, cols, :].rearrange("p i t -> p (i t)"))
+
+        xm_codes = [sb("xm_codes%d" % k, [P, PASSES, P], U32) for k in range(DBLOCKS)]
+        xm_scale = [sb("xm_scale%d" % k, [P, PASSES, P], U8) for k in range(DBLOCKS)]
+        xm_bf = [sb("xm_bf%d" % k, [P, PASSES, P, PACK], BF16) for k in range(DBLOCKS)]
+
+        def cast_xm(k):
+            for c in range(PASSES):
+                cols = slice((k % 2) * P, (k % 2 + 1) * P)
+                nc.scalar.copy(out=xm_bf[k][:, c].rearrange("p (q i) t -> p q t i", i=4),
+                               in_=xm_raw[c][k // 2][:, :, cols].rearrange("p t (q i) -> p q t i", i=4))
+
+        def quant_xm(k):
+            nc.vector.quantize_mx(out=xm_codes[k][:].rearrange("p c m -> p (c m)").bitcast(E4),
+                                  scales=xm_scale[k][:].rearrange("p c m -> p (c m)"),
+                                  in_=xm_bf[k][:].rearrange("p c m t -> p (c m t)"))
+
+        def product(k):
+            acc = psum.tile([P, N], F32, name="acc_d", tag="acc_d")
+            for c in range(PASSES):
+                nc.tensor.matmul_mx(out=acc[:], lhsT=xm_codes[k][:, c, :].bitcast(E4), lhsT_scale=xm_scale[k][:, c, :],
+                                    rhs=g_codes[c][:].bitcast(E5), rhs_scale=g_scale[c][:],
+                                    start=(c == 0), stop=(c == PASSES - 1))
+            dense = sb("dense%d" % k, [P, N], F32)
+            nc.scalar.copy(out=dense[:], in_=acc[:])
+            return dense
+
+        def place(k, dense):
+            window = windows[k % WINDOWS]
+            nc.vector.tensor_copy(window[:].indirect(offsets[:]), dense[:])
+            nc.sync.dma_start(out=out[k * P:(k + 1) * P, :], in_=window[:])
+
+        whole = slice(0, N)
+        halves = (slice(0, N // 2), slice(N // 2, N))
+
+        quant_xt(0)
+        nc.vector.tensor_copy(w_word_g[:], words[:].indirect(offsets[:]))
+        weigh_y(0, 0, False)
+        weigh_y(0, 1, False)
+        for t in range(PACK):
+            scores(0, t)
+        weigh_y(0, 2, True)
+        weigh_y(0, 3, True)
+        for t in range(PACK):
+            grad(0, t, whole)
+        quant_xt(1)
+        weigh_y(1, 0, False)
+        weigh_y(1, 1, False)
+        for t in range(PACK):
+            scores(1, t)
+        pack_g(0, whole, True)
+        weigh_y(1, 2, True)
+        quant_g(0, whole)
+        weigh_y(1, 3, True)
+        for t in range(PACK):
+            grad(1, t, halves[0])
+        cast_xm(0)
+        pack_g(1, halves[0], False)
+        for t in range(PACK):
+            grad(1, t, halves[1])
+        quant_xm(0)
+        pack_g(1, halves[1], True)
+        quant_g(1, halves[0])
+        quant_g(1, halves[1])
+        for k in range(WINDOWS):
+            nc.vector.memset(windows[k][:], 0.0)
+        dense = [None] * DBLOCKS
+        dense[0] = product(0)
+        cast_xm(1)
+        quant_xm(1)
+        dense[1] = product(1)
+        for k in range(DBLOCKS):
+            if k + 2 < DBLOCKS:
+                cast_xm(k + 2)
+            place(k, dense[k])
+            if k + 2 < DBLOCKS:
+                quant_xm(k + 2)
+                dense[k + 2] = product(k + 2)

@@ -11,8 +11,8 @@ I32 = mybir.dt.int32
 U32 = mybir.dt.uint32
 U16 = mybir.dt.uint16
 U8 = mybir.dt.uint8
-E4 = mybir.dt.float8_e4m3fn_x4
-E5 = mybir.dt.float8_e5m2_x4
+E4M3 = mybir.dt.float8_e4m3fn_x4
+E5M2 = mybir.dt.float8_e5m2_x4
 ACT = mybir.ActivationFunctionType
 ALU = mybir.AluOpType
 
@@ -21,24 +21,40 @@ PACK = 4
 KP = P * PACK
 PASSES = R // KP
 DBLOCKS = D // P
+BAND = 16
+QUAD = 32
+RUN = 4
+HALF = N // 2
+FIRST, SECOND, ALL = slice(0, HALF), slice(HALF, N), slice(0, N)
 WINDOWS = 3
-XT_V = (80, 64)
+PSUM_BUFS = 4
+XT0_VECTOR = 80
+SCALAR_WY = ((0, 3), (1, 1))
 
 
 def tile_attend_gnce_w_kernel(tc, xT, w_words, w_scales, y, wt, xm, offs, out):
     nc = tc.nc
     with ExitStack() as ctx:
         keep = ctx.enter_context(tc.tile_pool(name="keep", bufs=1))
-        psum = ctx.enter_context(tc.psum_pool(name="psum", bufs=4))
+        psum = ctx.enter_context(tc.psum_pool(name="psum", bufs=PSUM_BUFS))
 
         def sb(name, shape, dtype):
             return keep.tile(shape, dtype, name=name, align_bytes=64)
 
-        offsets = keep.tile([P, N // 16], U16, name="offsets")
+        def copy(on_vector, dst, src):
+            if on_vector:
+                nc.vector.tensor_copy(out=dst, in_=src)
+            else:
+                nc.scalar.copy(out=dst, in_=src)
+
+        def entries(slots):
+            return offsets[:, slots.start // BAND:slots.stop // BAND]
+
+        offsets = keep.tile([P, N // BAND], U16, name="offsets")
         nc.sync.dma_start(offsets[:], offs)
 
         xt_raw = [sb("xt_raw%d" % c, [P, PACK, KP], F32) for c in range(PASSES)]
-        y_raw = [[sb("y_raw%d%d" % (c, h), [P, 2, N], F32) for h in range(2)] for c in range(PASSES)]
+        y_raw = [sb("y_raw%d" % c, [P, PACK, N], F32) for c in range(PASSES)]
         xm_raw = [[sb("xm_raw%d%d" % (c, h), [P, PACK, D // 2], F32) for h in range(2)] for c in range(PASSES)]
         words = sb("words", [P, T], U32)
         scales = sb("scales", [P, T], U8)
@@ -47,163 +63,170 @@ def tile_attend_gnce_w_kernel(tc, xT, w_words, w_scales, y, wt, xm, offs, out):
         def load_xt(c):
             nc.sync.dma_start(out=xt_raw[c][:], in_=xT[0][:, c * KP:(c + 1) * KP].rearrange("(p j) r -> p j r", j=PACK))
 
-        def load_y(c):
-            rows = y[0][c * KP:(c + 1) * KP, :].rearrange("(p t) i -> p t i", t=PACK)
-            for h in range(2):
-                nc.sync.dma_start(out=y_raw[c][h][:], in_=rows[:, 2 * h:2 * h + 2, :])
-
-        def load_xm(h):
-            for c in range(PASSES):
-                rows = xm[0][c * KP:(c + 1) * KP, :].rearrange("(p t) d -> p t d", t=PACK)
-                nc.sync.dma_start(out=xm_raw[c][h][:], in_=rows[:, :, h * (D // 2):(h + 1) * (D // 2)])
-
         load_xt(0)
         nc.vector.memset(scales[:].bitcast(I32), 0)
-        for q in range(4):
-            nc.scalar.dma_start(out=scales[32 * q:32 * q + 4, :].bitcast(I32),
-                                in_=w_scales[0][4 * q:4 * q + 4, :].bitcast(I32))
         nc.scalar.dma_start(out=w_rows[:], in_=wt[0].rearrange("(c p t) o -> p c (t o)", p=P, t=PACK))
+        for q in range(P // QUAD):
+            nc.sync.dma_start(out=scales[QUAD * q:QUAD * q + 4, :].bitcast(I32),
+                              in_=w_scales[0][4 * q:4 * q + 4, :].bitcast(I32))
         nc.sync.dma_start(out=words[:].bitcast(I32), in_=w_words[0].rearrange("p n t -> p (n t)").bitcast(I32))
-        load_y(0)
         load_xt(1)
-        load_y(1)
-        load_xm(0)
-        load_xm(1)
+        for c in range(PASSES):
+            y_rows = y[0][c * KP:(c + 1) * KP, :].rearrange("(p t) i -> p t i", t=PACK)
+            for t in range(0, PACK, 2):
+                nc.sync.dma_start(out=y_raw[c][:, t:t + 2, :], in_=y_rows[:, t:t + 2, :])
+        for h in range(2):
+            for c in range(PASSES):
+                xm_rows = xm[0][c * KP:(c + 1) * KP, :].rearrange("(p t) d -> p t d", t=PACK)
+                nc.sync.dma_start(out=xm_raw[c][h][:], in_=xm_rows[:, :, h * (D // 2):(h + 1) * (D // 2)])
 
         warm = sb("warm", [P, 16], F32)
         nc.gpsimd.memset(warm[:], 0.0)
         nc.scalar.activation(out=warm[:, 8:9], in_=warm[:, 0:1], func=ACT.Sigmoid)
 
         windows = [sb("window%d" % k, [P, T], F32) for k in range(WINDOWS)]
+        for window in windows:
+            nc.vector.memset(window[:].bitcast(I32), 0)
 
         w_scale_g = sb("w_scale_g", [P, N], U8)
         w_word_g = sb("w_word_g", [P, N], U32)
-        nc.vector.tensor_copy(w_scale_g[:], scales[:].indirect(offsets[:]))
-
         xt_codes = [sb("xt_codes%d" % c, [P, KP], U32) for c in range(PASSES)]
         xt_scale = [sb("xt_scale%d" % c, [P, KP], U8) for c in range(PASSES)]
-        g_codes = [sb("g_codes%d" % c, [P, N], U32) for c in range(PASSES)]
-        g_scale = [sb("g_scale%d" % c, [P, N], U8) for c in range(PASSES)]
-        sig = [[None] * PACK for c in range(PASSES)]
-        wy = [[None] * PACK for c in range(PASSES)]
+        g_codes = [sb("g_codes%d" % c, [P, HALF + N], U32) for c in range(PASSES)]
+        g_scale = [sb("g_scale%d" % c, [P, HALF + N], U8) for c in range(PASSES)]
+        for c in range(PASSES):
+            nc.vector.memset(g_codes[c][:, :HALF].bitcast(I32), 0)
+            nc.vector.memset(g_scale[c][:, :HALF].bitcast(I32), 0)
+        sig = [[sb("sig%d%d" % (c, t), [P, N], F32) for t in range(PACK)] for c in range(PASSES)]
+        wy = [[sb("wy%d%d" % (c, t), [P, N], F32) for t in range(PACK)] for c in range(PASSES)]
         g_rows = [sb("g_rows%d" % c, [P, PACK, N], BF16) for c in range(PASSES)]
         g_packed = [sb("g_packed%d" % c, [P, N, PACK], BF16) for c in range(PASSES)]
+        xt_bf = [sb("xt_bf%d" % c, [P, PACK, P, PACK], BF16) for c in range(PASSES)]
+        xm_codes = sb("xm_codes", [P, DBLOCKS, PASSES, P], U32)
+        xm_scale = sb("xm_scale", [P, DBLOCKS, PASSES, P], U8)
+        xm_bf = sb("xm_bf", [P, DBLOCKS, PASSES, P, PACK], BF16)
+        dense = [sb("dense%d" % k, [P, N], F32) for k in range(DBLOCKS)]
+
+        def cast_xt(c, m0, m1, on_vector):
+            copy(on_vector, xt_bf[c][:].rearrange("p t m j -> p m j t")[:, m0:m1],
+                 xt_raw[c][:].rearrange("p j (m t) -> p m j t", t=PACK)[:, m0:m1])
 
         def quant_xt(c):
-            xb = sb("xt_bf%d" % c, [P, PACK, P, PACK], BF16)
-            dst = xb[:].rearrange("p t m j -> p m j t")
-            srcv = xt_raw[c][:].rearrange("p j (m t) -> p m j t", t=PACK)
-            mv = XT_V[c]
-            nc.vector.tensor_copy(out=dst[:, :mv], in_=srcv[:, :mv])
-            nc.scalar.copy(out=dst[:, mv:], in_=srcv[:, mv:])
-            nc.vector.quantize_mx(out=xt_codes[c][:].bitcast(E4), scales=xt_scale[c][:],
-                                  in_=xb[:].rearrange("p t m j -> p (t m j)"))
+            nc.vector.quantize_mx(out=xt_codes[c][:].bitcast(E4M3), scales=xt_scale[c][:],
+                                  in_=xt_bf[c][:].rearrange("p t m j -> p (t m j)"))
 
         def scores(c, t):
             acc = psum.tile([P, N], F32, name="acc_a", tag="acc_a")
             cols = slice(t * P, (t + 1) * P)
-            nc.tensor.matmul_mx(out=acc[:], lhsT=xt_codes[c][:, cols].bitcast(E4), lhsT_scale=xt_scale[c][:, cols],
-                                rhs=w_word_g[:].bitcast(E4), rhs_scale=w_scale_g[:], start=True, stop=True)
-            sig[c][t] = sb("sig%d%d" % (c, t), [P, N], F32)
+            nc.tensor.matmul_mx(out=acc[:], lhsT=xt_codes[c][:, cols].bitcast(E4M3), lhsT_scale=xt_scale[c][:, cols],
+                                rhs=w_word_g[:].bitcast(E4M3), rhs_scale=w_scale_g[:], start=True, stop=True)
             nc.scalar.activation(out=sig[c][t][:], in_=acc[:], func=ACT.Sigmoid)
 
-        def weigh_y(c, t, on_vector):
-            wy[c][t] = sb("wy%d%d" % (c, t), [P, N], F32)
-            src = y_raw[c][t // 2][:, t % 2, :]
-            if on_vector:
-                nc.vector.tensor_scalar_mul(wy[c][t][:], src, w_rows[:, c, t:t + 1])
+        def weigh_y(c, t):
+            if (c, t) in SCALAR_WY:
+                nc.scalar.activation(out=wy[c][t][:], in_=y_raw[c][:, t, :], func=ACT.Copy, scale=w_rows[:, c, t:t + 1])
             else:
-                nc.scalar.activation(out=wy[c][t][:], in_=src, func=ACT.Copy, scale=w_rows[:, c, t:t + 1])
+                nc.vector.tensor_scalar_mul(wy[c][t][:], y_raw[c][:, t, :], w_rows[:, c, t:t + 1])
 
-        def grad(c, t, cols):
-            nc.vector.scalar_tensor_tensor(out=g_rows[c][:, t, cols], in0=sig[c][t][:, cols], scalar=w_rows[:, c, t:t + 1],
-                                           in1=wy[c][t][:, cols], op0=ALU.mult, op1=ALU.subtract)
+        def grad(c, t, slots):
+            nc.vector.scalar_tensor_tensor(out=g_rows[c][:, t, slots], in0=sig[c][t][:, slots],
+                                           scalar=w_rows[:, c, t:t + 1], in1=wy[c][t][:, slots],
+                                           op0=ALU.mult, op1=ALU.subtract)
 
-        def pack_g(c, cols, on_vector):
-            dst = g_packed[c][:, cols, :].rearrange("p (q i) t -> p q t i", i=4)
-            srcv = g_rows[c][:, :, cols].rearrange("p t (q i) -> p q t i", i=4)
-            if on_vector:
-                nc.vector.tensor_copy(out=dst, in_=srcv)
-            else:
-                nc.scalar.copy(out=dst, in_=srcv)
+        def pack_g(c, slots, on_vector):
+            copy(on_vector, g_packed[c][:, slots, :].rearrange("p (q i) t -> p q t i", i=RUN),
+                 g_rows[c][:, :, slots].rearrange("p t (q i) -> p q t i", i=RUN))
 
-        def quant_g(c, cols):
-            nc.vector.quantize_mx(out=g_codes[c][:, cols].bitcast(E5), scales=g_scale[c][:, cols],
-                                  in_=g_packed[c][:, cols, :].rearrange("p i t -> p (i t)"))
+        def quant_g(c, slots):
+            cols = slice(HALF + slots.start, HALF + slots.stop)
+            nc.vector.quantize_mx(out=g_codes[c][:, cols].bitcast(E5M2), scales=g_scale[c][:, cols],
+                                  in_=g_packed[c][:, slots, :].rearrange("p i t -> p (i t)"))
 
-        xm_codes = [sb("xm_codes%d" % k, [P, PASSES, P], U32) for k in range(DBLOCKS)]
-        xm_scale = [sb("xm_scale%d" % k, [P, PASSES, P], U8) for k in range(DBLOCKS)]
-        xm_bf = [sb("xm_bf%d" % k, [P, PASSES, P, PACK], BF16) for k in range(DBLOCKS)]
+        def cast_xm(k, c, on_vector):
+            cols = slice((k % 2) * P, (k % 2 + 1) * P)
+            copy(on_vector, xm_bf[:, k, c].rearrange("p (q i) t -> p q t i", i=RUN),
+                 xm_raw[c][k // 2][:, :, cols].rearrange("p t (q i) -> p q t i", i=RUN))
 
-        def cast_xm(k):
-            for c in range(PASSES):
-                cols = slice((k % 2) * P, (k % 2 + 1) * P)
-                nc.scalar.copy(out=xm_bf[k][:, c].rearrange("p (q i) t -> p q t i", i=4),
-                               in_=xm_raw[c][k // 2][:, :, cols].rearrange("p t (q i) -> p q t i", i=4))
+        def quant_xm(k0, k1):
+            nc.vector.quantize_mx(out=xm_codes[:, k0:k1].rearrange("p k c m -> p (k c m)").bitcast(E4M3),
+                                  scales=xm_scale[:, k0:k1].rearrange("p k c m -> p (k c m)"),
+                                  in_=xm_bf[:, k0:k1].rearrange("p k c m t -> p (k c m t)"))
 
-        def quant_xm(k):
-            nc.vector.quantize_mx(out=xm_codes[k][:].rearrange("p c m -> p (c m)").bitcast(E4),
-                                  scales=xm_scale[k][:].rearrange("p c m -> p (c m)"),
-                                  in_=xm_bf[k][:].rearrange("p c m t -> p (c m t)"))
-
-        def product(k):
+        def product(k, first_col):
             acc = psum.tile([P, N], F32, name="acc_d", tag="acc_d")
+            cols = slice(first_col, first_col + N)
             for c in range(PASSES):
-                nc.tensor.matmul_mx(out=acc[:], lhsT=xm_codes[k][:, c, :].bitcast(E4), lhsT_scale=xm_scale[k][:, c, :],
-                                    rhs=g_codes[c][:].bitcast(E5), rhs_scale=g_scale[c][:],
+                nc.tensor.matmul_mx(out=acc[:], lhsT=xm_codes[:, k, c, :].bitcast(E4M3), lhsT_scale=xm_scale[:, k, c, :],
+                                    rhs=g_codes[c][:, cols].bitcast(E5M2), rhs_scale=g_scale[c][:, cols],
                                     start=(c == 0), stop=(c == PASSES - 1))
-            dense = sb("dense%d" % k, [P, N], F32)
-            nc.scalar.copy(out=dense[:], in_=acc[:])
-            return dense
+            return acc
 
-        def place(k, dense):
+        def leave(k, slots, sums):
+            nc.scalar.copy(out=dense[k][:, slots], in_=sums)
+
+        def place(k, slots):
             window = windows[k % WINDOWS]
-            nc.vector.tensor_copy(window[:].indirect(offsets[:]), dense[:])
-            nc.sync.dma_start(out=out[k * P:(k + 1) * P, :], in_=window[:])
+            nc.vector.tensor_copy(window[:].indirect(entries(slots)), dense[k][:, slots])
+            rows = out[k * P:(k + 1) * P, :]
+            if slots.stop == N and k < DBLOCKS - 1:
+                nc.sync.dma_start(out=rows, in_=window[:])
+            elif slots.stop == N:
+                nc.sync.dma_start(out=rows[:, :T // 2], in_=window[:, :T // 2])
+                nc.scalar.dma_start(out=rows[:, T // 2:], in_=window[:, T // 2:])
 
-        whole = slice(0, N)
-        halves = (slice(0, N // 2), slice(N // 2, N))
-
+        cast_xt(0, 0, XT0_VECTOR, True)
+        cast_xt(0, XT0_VECTOR, P, False)
+        nc.vector.tensor_copy(w_scale_g[:], scales[:].indirect(entries(ALL)))
         quant_xt(0)
-        nc.vector.tensor_copy(w_word_g[:], words[:].indirect(offsets[:]))
-        weigh_y(0, 0, False)
-        weigh_y(0, 1, False)
+        nc.vector.tensor_copy(w_word_g[:], words[:].indirect(entries(ALL)))
         for t in range(PACK):
             scores(0, t)
-        weigh_y(0, 2, True)
-        weigh_y(0, 3, True)
-        for t in range(PACK):
-            grad(0, t, whole)
+        cast_xt(1, 0, P, True)
         quant_xt(1)
-        weigh_y(1, 0, False)
-        weigh_y(1, 1, False)
+        for c in range(PASSES):
+            for t in range(PACK):
+                weigh_y(c, t)
         for t in range(PACK):
             scores(1, t)
-        pack_g(0, whole, True)
-        weigh_y(1, 2, True)
-        quant_g(0, whole)
-        weigh_y(1, 3, True)
+
         for t in range(PACK):
-            grad(1, t, halves[0])
-        cast_xm(0)
-        pack_g(1, halves[0], False)
+            grad(0, t, ALL)
         for t in range(PACK):
-            grad(1, t, halves[1])
-        quant_xm(0)
-        pack_g(1, halves[1], True)
-        quant_g(1, halves[0])
-        quant_g(1, halves[1])
-        for k in range(WINDOWS):
-            nc.vector.memset(windows[k][:], 0.0)
-        dense = [None] * DBLOCKS
-        dense[0] = product(0)
-        cast_xm(1)
-        quant_xm(1)
-        dense[1] = product(1)
-        for k in range(DBLOCKS):
-            if k + 2 < DBLOCKS:
-                cast_xm(k + 2)
-            place(k, dense[k])
-            if k + 2 < DBLOCKS:
-                quant_xm(k + 2)
-                dense[k + 2] = product(k + 2)
+            grad(1, t, FIRST)
+        cast_xm(0, 0, False)
+        cast_xm(0, 1, True)
+        pack_g(0, FIRST, False)
+        pack_g(1, FIRST, True)
+        for c in range(PASSES):
+            cast_xm(1, c, False)
+        for c in range(PASSES):
+            quant_g(c, FIRST)
+        quant_xm(0, 1)
+        early0 = product(0, 0)
+
+        for t in range(PACK):
+            grad(1, t, SECOND)
+        pack_g(0, SECOND, False)
+        quant_xm(1, 2)
+        pack_g(1, SECOND, True)
+        for c in range(PASSES):
+            quant_g(c, SECOND)
+        leave(0, FIRST, early0[:, HALF:])
+        early1 = product(1, 0)
+
+        leave(0, SECOND, product(0, HALF)[:, SECOND])
+        for c in range(PASSES):
+            cast_xm(2, c, False)
+        leave(1, FIRST, early1[:, HALF:])
+        place(0, FIRST)
+        for c in range(PASSES):
+            cast_xm(3, c, False)
+        quant_xm(2, DBLOCKS)
+        leave(1, SECOND, product(1, HALF)[:, SECOND])
+        place(1, FIRST)
+        for k in range(2, DBLOCKS):
+            leave(k, ALL, product(k, HALF)[:])
+        place(0, SECOND)
+        place(1, SECOND)
+        for k in range(2, DBLOCKS):
+            place(k, ALL)

@@ -26,23 +26,19 @@ QUAD = 32
 RUN = 4
 HALF = N // 2
 FIRST, SECOND, ALL = slice(0, HALF), slice(HALF, N), slice(0, N)
-WINDOWS = 3
-PSUM_BUFS = 4
-XT0_VECTOR = 80
-SCALAR_WY = ((0, 3), (1, 1))
 
 
 def tile_attend_gnce_w_kernel(tc, xT, w_words, w_scales, y, wt, xm, offs, out):
     nc = tc.nc
     with ExitStack() as ctx:
         keep = ctx.enter_context(tc.tile_pool(name="keep", bufs=1))
-        psum = ctx.enter_context(tc.psum_pool(name="psum", bufs=PSUM_BUFS))
+        psum = ctx.enter_context(tc.psum_pool(name="psum", bufs=2))
 
-        def sb(name, shape, dtype):
-            return keep.tile(shape, dtype, name=name, align_bytes=64)
+        def sb(name, shape, dtype, tag=""):
+            return keep.tile(shape, dtype, name=name, tag=tag or name, align_bytes=64)
 
-        def copy(on_vector, dst, src):
-            if on_vector:
+        def copy(engine, dst, src):
+            if engine:
                 nc.vector.tensor_copy(out=dst, in_=src)
             else:
                 nc.scalar.copy(out=dst, in_=src)
@@ -51,8 +47,6 @@ def tile_attend_gnce_w_kernel(tc, xT, w_words, w_scales, y, wt, xm, offs, out):
             return offsets[:, slots.start // BAND:slots.stop // BAND]
 
         offsets = keep.tile([P, N // BAND], U16, name="offsets")
-        nc.sync.dma_start(offsets[:], offs)
-
         xt_raw = [sb("xt_raw%d" % c, [P, PACK, KP], F32) for c in range(PASSES)]
         y_raw = [sb("y_raw%d" % c, [P, PACK, N], F32) for c in range(PASSES)]
         xm_raw = [[sb("xm_raw%d%d" % (c, h), [P, PACK, D // 2], F32) for h in range(2)] for c in range(PASSES)]
@@ -63,97 +57,123 @@ def tile_attend_gnce_w_kernel(tc, xT, w_words, w_scales, y, wt, xm, offs, out):
         def load_xt(c):
             nc.sync.dma_start(out=xt_raw[c][:], in_=xT[0][:, c * KP:(c + 1) * KP].rearrange("(p j) r -> p j r", j=PACK))
 
-        load_xt(0)
-        nc.vector.memset(scales[:].bitcast(I32), 0)
-        nc.scalar.dma_start(out=w_rows[:], in_=wt[0].rearrange("(c p t) o -> p c (t o)", p=P, t=PACK))
-        for q in range(P // QUAD):
-            nc.sync.dma_start(out=scales[QUAD * q:QUAD * q + 4, :].bitcast(I32),
-                              in_=w_scales[0][4 * q:4 * q + 4, :].bitcast(I32))
-        nc.sync.dma_start(out=words[:].bitcast(I32), in_=w_words[0].rearrange("p n t -> p (n t)").bitcast(I32))
-        load_xt(1)
-        for c in range(PASSES):
+        def load_scales(queue):
+            nc.vector.memset(scales[:].bitcast(I32), 0)
+            for q in range(P // QUAD):
+                queue.dma_start(out=scales[QUAD * q:QUAD * q + 4, :].bitcast(I32),
+                                  in_=w_scales[0][4 * q:4 * q + 4, :].bitcast(I32))
+
+        def load_words():
+            nc.sync.dma_start(out=words[:].bitcast(I32), in_=w_words[0].rearrange("p n t -> p (n t)").bitcast(I32))
+
+        def load_w(queue):
+            queue.dma_start(out=w_rows[:], in_=wt[0].rearrange("(c p t) o -> p c (t o)", p=P, t=PACK))
+
+        def load_y(c, t0, t1, slots):
             y_rows = y[0][c * KP:(c + 1) * KP, :].rearrange("(p t) i -> p t i", t=PACK)
-            for t in range(0, PACK, 2):
-                nc.sync.dma_start(out=y_raw[c][:, t:t + 2, :], in_=y_rows[:, t:t + 2, :])
-        for h in range(2):
-            for c in range(PASSES):
-                xm_rows = xm[0][c * KP:(c + 1) * KP, :].rearrange("(p t) d -> p t d", t=PACK)
-                nc.sync.dma_start(out=xm_raw[c][h][:], in_=xm_rows[:, :, h * (D // 2):(h + 1) * (D // 2)])
+            nc.sync.dma_start(out=y_raw[c][:, t0:t1, slots], in_=y_rows[:, t0:t1, slots])
+
+        def load_xm(c, h):
+            rows = xm[0][c * KP:(c + 1) * KP, h * (D // 2):(h + 1) * (D // 2)]
+            nc.sync.dma_start(out=xm_raw[c][h][:], in_=rows.rearrange("(p t) d -> p t d", t=PACK))
+
+        nc.sync.dma_start(offsets[:], offs)
+        load_xt(0)
+        load_scales(nc.sync)
+        load_w(nc.scalar)
+        load_words()
+        load_xt(1)
+        load_y(0, 0, 2, ALL)
+        load_y(0, 2, 4, ALL)
+        load_y(1, 0, 2, ALL)
+        load_y(1, 2, 4, ALL)
+        load_xm(0, 0)
+        load_xm(1, 0)
+        load_xm(0, 1)
+        load_xm(1, 1)
 
         warm = sb("warm", [P, 16], F32)
-        nc.gpsimd.memset(warm[:], 0.0)
+        nc.vector.memset(warm[:], 0.0)
         nc.scalar.activation(out=warm[:, 8:9], in_=warm[:, 0:1], func=ACT.Sigmoid)
 
-        windows = [sb("window%d" % k, [P, T], F32) for k in range(WINDOWS)]
-        for window in windows:
-            nc.vector.memset(window[:].bitcast(I32), 0)
-
-        w_scale_g = sb("w_scale_g", [P, N], U8)
-        w_word_g = sb("w_word_g", [P, N], U32)
-        xt_codes = [sb("xt_codes%d" % c, [P, KP], U32) for c in range(PASSES)]
-        xt_scale = [sb("xt_scale%d" % c, [P, KP], U8) for c in range(PASSES)]
         g_codes = [sb("g_codes%d" % c, [P, HALF + N], U32) for c in range(PASSES)]
         g_scale = [sb("g_scale%d" % c, [P, HALF + N], U8) for c in range(PASSES)]
+        windows = [sb("window%d" % k, [P, T], F32) for k in range(3)]
+        for window in windows:
+            nc.vector.memset(window[:].bitcast(I32), 0)
         for c in range(PASSES):
             nc.vector.memset(g_codes[c][:, :HALF].bitcast(I32), 0)
             nc.vector.memset(g_scale[c][:, :HALF].bitcast(I32), 0)
+
+        w_scale_g = sb("w_scale_g", [P, N], U8)
+        w_word_g = sb("w_word_g", [P, N], U32)
+        xt_bf = [sb("xt_bf%d" % c, [P, PACK, P, PACK], BF16) for c in range(PASSES)]
+        xt_codes = [sb("xt_codes%d" % c, [P, KP], U32) for c in range(PASSES)]
+        xt_scale = [sb("xt_scale%d" % c, [P, KP], U8) for c in range(PASSES)]
         sig = [[sb("sig%d%d" % (c, t), [P, N], F32) for t in range(PACK)] for c in range(PASSES)]
         wy = [[sb("wy%d%d" % (c, t), [P, N], F32) for t in range(PACK)] for c in range(PASSES)]
         g_rows = [sb("g_rows%d" % c, [P, PACK, N], BF16) for c in range(PASSES)]
-        g_packed = [sb("g_packed%d" % c, [P, N, PACK], BF16) for c in range(PASSES)]
-        xt_bf = [sb("xt_bf%d" % c, [P, PACK, P, PACK], BF16) for c in range(PASSES)]
+        g_packed = [[sb("g_packed%d%d" % (c, h), [P, HALF, PACK], BF16) for h in range(2)] for c in range(PASSES)]
         xm_codes = sb("xm_codes", [P, DBLOCKS, PASSES, P], U32)
         xm_scale = sb("xm_scale", [P, DBLOCKS, PASSES, P], U8)
-        xm_bf = sb("xm_bf", [P, DBLOCKS, PASSES, P, PACK], BF16)
+        xm_bf = [sb("xm_bf0", [P, 2, PASSES, P, PACK], BF16)]
         dense = [sb("dense%d" % k, [P, N], F32) for k in range(DBLOCKS)]
+
+        def gather_scales():
+            nc.vector.tensor_copy(w_scale_g[:], scales[:].indirect(entries(ALL)))
+
+        def gather_words(slots):
+            nc.vector.tensor_copy(w_word_g[:, slots], words[:].indirect(entries(slots)))
 
         def cast_xt(c, m0, m1, on_vector):
             copy(on_vector, xt_bf[c][:].rearrange("p t m j -> p m j t")[:, m0:m1],
                  xt_raw[c][:].rearrange("p j (m t) -> p m j t", t=PACK)[:, m0:m1])
 
-        def quant_xt(c):
-            nc.vector.quantize_mx(out=xt_codes[c][:].bitcast(E4M3), scales=xt_scale[c][:],
-                                  in_=xt_bf[c][:].rearrange("p t m j -> p (t m j)"))
+        def quant_xt(c, t0, t1):
+            nc.vector.quantize_mx(out=xt_codes[c][:, t0 * P:t1 * P].bitcast(E4M3), scales=xt_scale[c][:, t0 * P:t1 * P],
+                                  in_=xt_bf[c][:, t0:t1].rearrange("p t m j -> p (t m j)"))
 
-        def scores(c, t):
-            acc = psum.tile([P, N], F32, name="acc_a", tag="acc_a")
+        def scores(c, t, slots, sign):
+            acc = psum.tile([P, slots.stop - slots.start], F32, name="acc_a", tag="acc_a", bufs=4)
             cols = slice(t * P, (t + 1) * P)
             nc.tensor.matmul_mx(out=acc[:], lhsT=xt_codes[c][:, cols].bitcast(E4M3), lhsT_scale=xt_scale[c][:, cols],
-                                rhs=w_word_g[:].bitcast(E4M3), rhs_scale=w_scale_g[:], start=True, stop=True)
-            nc.scalar.activation(out=sig[c][t][:], in_=acc[:], func=ACT.Sigmoid)
+                                rhs=w_word_g[:, slots].bitcast(E4M3), rhs_scale=w_scale_g[:, slots], start=True, stop=True)
+            nc.scalar.activation(out=sig[c][t][:, slots], in_=acc[:], func=ACT.Sigmoid, scale=sign)
 
-        def weigh_y(c, t):
-            if (c, t) in SCALAR_WY:
-                nc.scalar.activation(out=wy[c][t][:], in_=y_raw[c][:, t, :], func=ACT.Copy, scale=w_rows[:, c, t:t + 1])
+        def weigh_y(c, t, slots, on_vector):
+            if on_vector:
+                nc.vector.tensor_scalar_mul(wy[c][t][:, slots], y_raw[c][:, t, slots], w_rows[:, c, t:t + 1])
             else:
-                nc.vector.tensor_scalar_mul(wy[c][t][:], y_raw[c][:, t, :], w_rows[:, c, t:t + 1])
+                nc.scalar.activation(out=wy[c][t][:, slots], in_=y_raw[c][:, t, slots], func=ACT.Copy,
+                                     scale=w_rows[:, c, t:t + 1])
 
         def grad(c, t, slots):
             nc.vector.scalar_tensor_tensor(out=g_rows[c][:, t, slots], in0=sig[c][t][:, slots],
                                            scalar=w_rows[:, c, t:t + 1], in1=wy[c][t][:, slots],
                                            op0=ALU.mult, op1=ALU.subtract)
 
-        def pack_g(c, slots, on_vector):
-            copy(on_vector, g_packed[c][:, slots, :].rearrange("p (q i) t -> p q t i", i=RUN),
+        def pack_g(c, h, on_vector):
+            slots = slice(h * HALF, (h + 1) * HALF)
+            copy(on_vector, g_packed[c][h][:].rearrange("p (q i) t -> p q t i", i=RUN),
                  g_rows[c][:, :, slots].rearrange("p t (q i) -> p q t i", i=RUN))
 
-        def quant_g(c, slots):
-            cols = slice(HALF + slots.start, HALF + slots.stop)
+        def quant_g(c, h):
+            cols = slice(HALF + h * HALF, HALF + (h + 1) * HALF)
             nc.vector.quantize_mx(out=g_codes[c][:, cols].bitcast(E5M2), scales=g_scale[c][:, cols],
-                                  in_=g_packed[c][:, slots, :].rearrange("p i t -> p (i t)"))
+                                  in_=g_packed[c][h][:].rearrange("p i t -> p (i t)"))
 
         def cast_xm(k, c, on_vector):
             cols = slice((k % 2) * P, (k % 2 + 1) * P)
-            copy(on_vector, xm_bf[:, k, c].rearrange("p (q i) t -> p q t i", i=RUN),
+            copy(on_vector, xm_bf[k // 2][:, k % 2, c].rearrange("p (q i) t -> p q t i", i=RUN),
                  xm_raw[c][k // 2][:, :, cols].rearrange("p t (q i) -> p q t i", i=RUN))
 
         def quant_xm(k0, k1):
             nc.vector.quantize_mx(out=xm_codes[:, k0:k1].rearrange("p k c m -> p (k c m)").bitcast(E4M3),
                                   scales=xm_scale[:, k0:k1].rearrange("p k c m -> p (k c m)"),
-                                  in_=xm_bf[:, k0:k1].rearrange("p k c m t -> p (k c m t)"))
+                                  in_=xm_bf[k0 // 2][:, k0 % 2:(k1 - 1) % 2 + 1].rearrange("p k c m t -> p (k c m t)"))
 
         def product(k, first_col):
-            acc = psum.tile([P, N], F32, name="acc_d", tag="acc_d")
+            acc = psum.tile([P, N], F32, name="acc_d", tag="acc_d", bufs=4)
             cols = slice(first_col, first_col + N)
             for c in range(PASSES):
                 nc.tensor.matmul_mx(out=acc[:], lhsT=xm_codes[:, k, c, :].bitcast(E4M3), lhsT_scale=xm_scale[:, k, c, :],
@@ -165,64 +185,68 @@ def tile_attend_gnce_w_kernel(tc, xT, w_words, w_scales, y, wt, xm, offs, out):
             nc.scalar.copy(out=dense[k][:, slots], in_=sums)
 
         def place(k, slots):
-            window = windows[k % WINDOWS]
+            window = windows[k % 3]
             nc.vector.tensor_copy(window[:].indirect(entries(slots)), dense[k][:, slots])
-            rows = out[k * P:(k + 1) * P, :]
-            if slots.stop == N and k < DBLOCKS - 1:
-                nc.sync.dma_start(out=rows, in_=window[:])
-            elif slots.stop == N:
-                nc.sync.dma_start(out=rows[:, :T // 2], in_=window[:, :T // 2])
-                nc.scalar.dma_start(out=rows[:, T // 2:], in_=window[:, T // 2:])
+            if slots.stop == N:
+                nc.sync.dma_start(out=out[k * P:(k + 1) * P, :], in_=window[:])
 
-        cast_xt(0, 0, XT0_VECTOR, True)
-        cast_xt(0, XT0_VECTOR, P, False)
-        nc.vector.tensor_copy(w_scale_g[:], scales[:].indirect(entries(ALL)))
-        quant_xt(0)
-        nc.vector.tensor_copy(w_word_g[:], words[:].indirect(entries(ALL)))
-        for t in range(PACK):
-            scores(0, t)
+        cast_xt(0, 0, 80, True)
+        cast_xt(0, 80, P, False)
+        gather_scales()
+        quant_xt(0, 0, 4)
+        gather_words(FIRST)
+        gather_words(SECOND)
+        scores(0, 0, FIRST, 1.0)
+        scores(0, 1, FIRST, 1.0)
+        scores(0, 0, SECOND, 1.0)
+        scores(0, 1, SECOND, 1.0)
+        for t in range(2, PACK):
+            scores(0, t, ALL, 1.0)
         cast_xt(1, 0, P, True)
-        quant_xt(1)
-        for c in range(PASSES):
-            for t in range(PACK):
-                weigh_y(c, t)
+        quant_xt(1, 0, 2)
+        quant_xt(1, 2, 4)
         for t in range(PACK):
-            scores(1, t)
-
+            weigh_y(0, t, ALL, t in (0, 2))
+        for t in range(PACK):
+            scores(1, t, ALL, 1.0)
+        for t in range(PACK):
+            weigh_y(1, t, ALL, True)
         for t in range(PACK):
             grad(0, t, ALL)
         for t in range(PACK):
             grad(1, t, FIRST)
+        pack_g(0, 0, False)
         cast_xm(0, 0, False)
         cast_xm(0, 1, True)
-        pack_g(0, FIRST, False)
-        pack_g(1, FIRST, True)
-        for c in range(PASSES):
-            cast_xm(1, c, False)
-        for c in range(PASSES):
-            quant_g(c, FIRST)
+        pack_g(1, 0, True)
+        quant_g(0, 0)
+        quant_g(1, 0)
         quant_xm(0, 1)
         early0 = product(0, 0)
-
         for t in range(PACK):
             grad(1, t, SECOND)
-        pack_g(0, SECOND, False)
-        quant_xm(1, 2)
-        pack_g(1, SECOND, True)
+        pack_g(0, 1, False)
         for c in range(PASSES):
-            quant_g(c, SECOND)
+            cast_xm(1, c, False)
+        quant_xm(1, 2)
         leave(0, FIRST, early0[:, HALF:])
+        pack_g(1, 1, False)
+        quant_g(0, 1)
+        quant_g(1, 1)
         early1 = product(1, 0)
-
-        leave(0, SECOND, product(0, HALF)[:, SECOND])
+        leave(1, FIRST, early1[:, HALF:])
+        full0 = product(0, HALF)
+        place(0, FIRST)
+        xm_bf.append(sb("xm_bf1", [P, 2, PASSES, P, PACK], BF16, tag="g_rows1"))
         for c in range(PASSES):
             cast_xm(2, c, False)
-        leave(1, FIRST, early1[:, HALF:])
-        place(0, FIRST)
+        quant_xm(2, 3)
+        leave(0, SECOND, full0[:, SECOND])
+        full1 = product(1, HALF)
         for c in range(PASSES):
             cast_xm(3, c, False)
-        quant_xm(2, DBLOCKS)
-        leave(1, SECOND, product(1, HALF)[:, SECOND])
+        quant_xm(3, 4)
+        leave(1, SECOND, full1[:, SECOND])
         place(1, FIRST)
         for k in range(2, DBLOCKS):
             leave(k, ALL, product(k, HALF)[:])

@@ -59,9 +59,8 @@ def tile_attend_gnce_w_kernel(tc, xT, w_words, w_scales, y, wt, xm, offs, out):
 
         def load_scales(queue):
             nc.vector.memset(scales[:].bitcast(I32), 0)
-            for q in range(P // QUAD):
-                queue.dma_start(out=scales[QUAD * q:QUAD * q + 4, :].bitcast(I32),
-                                  in_=w_scales[0][4 * q:4 * q + 4, :].bitcast(I32))
+            for f in range(4):
+                queue.dma_start(out=scales[f:P:QUAD, :].bitcast(I32), in_=w_scales[0][f:16:4, :].bitcast(I32))
 
         def load_words():
             nc.sync.dma_start(out=words[:].bitcast(I32), in_=w_words[0].rearrange("p n t -> p (n t)").bitcast(I32))
@@ -77,8 +76,8 @@ def tile_attend_gnce_w_kernel(tc, xT, w_words, w_scales, y, wt, xm, offs, out):
             rows = xm[0][c * KP:(c + 1) * KP, h * (D // 2):(h + 1) * (D // 2)]
             nc.sync.dma_start(out=xm_raw[c][h][:], in_=rows.rearrange("(p t) d -> p t d", t=PACK))
 
-        nc.sync.dma_start(offsets[:], offs)
         load_xt(0)
+        nc.sync.dma_start(offsets[:], offs)
         load_scales(nc.sync)
         load_w(nc.scalar)
         load_words()
@@ -220,8 +219,8 @@ def tile_attend_gnce_w_kernel(tc, xT, w_words, w_scales, y, wt, xm, offs, out):
         cast_xm(0, 1, True)
         pack_g(1, 0, True)
         quant_g(0, 0)
-        quant_g(1, 0)
         quant_xm(0, 1)
+        quant_g(1, 0)
         early0 = product(0, 0)
         for t in range(PACK):
             grad(1, t, SECOND)

@@ -91,10 +91,6 @@ def tile_attend_gnce_w_kernel(tc, xT, w_words, w_scales, y, wt, xm, offs, out):
         load_xm(0, 1)
         load_xm(1, 1)
 
-        warm = sb("warm", [P, 16], F32)
-        nc.vector.memset(warm[:], 0.0)
-        nc.scalar.activation(out=warm[:, 8:9], in_=warm[:, 0:1], func=ACT.Sigmoid)
-
         g_codes = [sb("g_codes%d" % c, [P, HALF + N], U32) for c in range(PASSES)]
         g_scale = [sb("g_scale%d" % c, [P, HALF + N], U8) for c in range(PASSES)]
         windows = [sb("window%d" % k, [P, T], F32) for k in range(3)]
@@ -111,12 +107,12 @@ def tile_attend_gnce_w_kernel(tc, xT, w_words, w_scales, y, wt, xm, offs, out):
         xt_scale = [sb("xt_scale%d" % c, [P, KP], U8) for c in range(PASSES)]
         sig = [[sb("sig%d%d" % (c, t), [P, N], F32) for t in range(PACK)] for c in range(PASSES)]
         wy = [[sb("wy%d%d" % (c, t), [P, N], F32) for t in range(PACK)] for c in range(PASSES)]
-        g_rows = [sb("g_rows%d" % c, [P, PACK, N], BF16) for c in range(PASSES)]
-        g_packed = [[sb("g_packed%d%d" % (c, h), [P, HALF, PACK], BF16) for h in range(2)] for c in range(PASSES)]
+        g_rows = {(0, 0): sb("g_rows0", [P, PACK, N], BF16), (1, 0): sb("g_rows10", [P, PACK, HALF], BF16)}
+        g_packed = [[sb("g_packed%d0" % c, [P, HALF, PACK], BF16)] for c in range(PASSES)]
         xm_codes = sb("xm_codes", [P, DBLOCKS, PASSES, P], U32)
         xm_scale = sb("xm_scale", [P, DBLOCKS, PASSES, P], U8)
-        xm_bf = [sb("xm_bf0", [P, 2, PASSES, P, PACK], BF16)]
-        dense = [sb("dense%d" % k, [P, N], F32) for k in range(DBLOCKS)]
+        xm_bf = [sb("xm_bf%d" % k, [P, PASSES, P, PACK], BF16) for k in range(2)]
+        dense = {k: sb("dense%d" % k, [P, N], F32) for k in (0, 2, 3)}
 
         def gather_scales():
             nc.vector.tensor_copy(w_scale_g[:], scales[:].indirect(entries(ALL)))
@@ -146,15 +142,20 @@ def tile_attend_gnce_w_kernel(tc, xT, w_words, w_scales, y, wt, xm, offs, out):
                 nc.scalar.activation(out=wy[c][t][:, slots], in_=y_raw[c][:, t, slots], func=ACT.Copy,
                                      scale=w_rows[:, c, t:t + 1])
 
+        def rows_of_g(c, slots):
+            if c == 0:
+                return g_rows[0, 0][:, :, slots]
+            return g_rows[1, slots.start // HALF][:]
+
         def grad(c, t, slots):
-            nc.vector.scalar_tensor_tensor(out=g_rows[c][:, t, slots], in0=sig[c][t][:, slots],
+            nc.vector.scalar_tensor_tensor(out=rows_of_g(c, slots)[:, t, :], in0=sig[c][t][:, slots],
                                            scalar=w_rows[:, c, t:t + 1], in1=wy[c][t][:, slots],
                                            op0=ALU.mult, op1=ALU.subtract)
 
         def pack_g(c, h, on_vector):
             slots = slice(h * HALF, (h + 1) * HALF)
             copy(on_vector, g_packed[c][h][:].rearrange("p (q i) t -> p q t i", i=RUN),
-                 g_rows[c][:, :, slots].rearrange("p t (q i) -> p q t i", i=RUN))
+                 rows_of_g(c, slots).rearrange("p t (q i) -> p q t i", i=RUN))
 
         def quant_g(c, h):
             cols = slice(HALF + h * HALF, HALF + (h + 1) * HALF)
@@ -163,13 +164,13 @@ def tile_attend_gnce_w_kernel(tc, xT, w_words, w_scales, y, wt, xm, offs, out):
 
         def cast_xm(k, c, on_vector):
             cols = slice((k % 2) * P, (k % 2 + 1) * P)
-            copy(on_vector, xm_bf[k // 2][:, k % 2, c].rearrange("p (q i) t -> p q t i", i=RUN),
+            copy(on_vector, xm_bf[k][:, c].rearrange("p (q i) t -> p q t i", i=RUN),
                  xm_raw[c][k // 2][:, :, cols].rearrange("p t (q i) -> p q t i", i=RUN))
 
-        def quant_xm(k0, k1):
-            nc.vector.quantize_mx(out=xm_codes[:, k0:k1].rearrange("p k c m -> p (k c m)").bitcast(E4M3),
-                                  scales=xm_scale[:, k0:k1].rearrange("p k c m -> p (k c m)"),
-                                  in_=xm_bf[k0 // 2][:, k0 % 2:(k1 - 1) % 2 + 1].rearrange("p k c m t -> p (k c m t)"))
+        def quant_xm(k, c0, c1):
+            nc.vector.quantize_mx(out=xm_codes[:, k, c0:c1].rearrange("p c m -> p (c m)").bitcast(E4M3),
+                                  scales=xm_scale[:, k, c0:c1].rearrange("p c m -> p (c m)"),
+                                  in_=xm_bf[k][:, c0:c1].rearrange("p c m t -> p (c m t)"))
 
         def product(k, first_col):
             acc = psum.tile([P, N], F32, name="acc_d", tag="acc_d", bufs=4)
@@ -219,32 +220,38 @@ def tile_attend_gnce_w_kernel(tc, xT, w_words, w_scales, y, wt, xm, offs, out):
         cast_xm(0, 1, True)
         pack_g(1, 0, True)
         quant_g(0, 0)
-        quant_xm(0, 1)
+        quant_xm(0, 0, 1)
+        quant_xm(0, 1, 2)
         quant_g(1, 0)
         early0 = product(0, 0)
+        g_rows[1, 1] = sb("g_rows11", [P, PACK, HALF], BF16, tag="xm_bf0")
         for t in range(PACK):
             grad(1, t, SECOND)
-        pack_g(0, 1, False)
         for c in range(PASSES):
             cast_xm(1, c, False)
-        quant_xm(1, 2)
+        quant_xm(1, 0, 2)
+        g_packed[0].append(sb("g_packed01", [P, HALF, PACK], BF16, tag="xm_raw10"))
+        g_packed[1].append(sb("g_packed11", [P, HALF, PACK], BF16))
+        pack_g(0, 1, False)
         leave(0, FIRST, early0[:, HALF:])
         pack_g(1, 1, False)
         quant_g(0, 1)
         quant_g(1, 1)
         early1 = product(1, 0)
+        dense[1] = sb("dense1", [P, N], F32, tag="xm_bf0")
         leave(1, FIRST, early1[:, HALF:])
         full0 = product(0, HALF)
         place(0, FIRST)
-        xm_bf.append(sb("xm_bf1", [P, 2, PASSES, P, PACK], BF16, tag="g_rows1"))
+        xm_late = sb("xm_late", [P, 2, PASSES, P, PACK], BF16, tag="g_packed11")
+        xm_bf.extend(xm_late[:, k] for k in range(2))
         for c in range(PASSES):
             cast_xm(2, c, False)
-        quant_xm(2, 3)
+        quant_xm(2, 0, 2)
         leave(0, SECOND, full0[:, SECOND])
         full1 = product(1, HALF)
         for c in range(PASSES):
             cast_xm(3, c, False)
-        quant_xm(3, 4)
+        quant_xm(3, 0, 2)
         leave(1, SECOND, full1[:, SECOND])
         place(1, FIRST)
         for k in range(2, DBLOCKS):

@@ -24,8 +24,12 @@ DBLOCKS = D // P
 BAND = 16
 QUAD = 32
 RUN = 4
+PAIR = 2
 HALF = N // 2
 FIRST, SECOND, ALL = slice(0, HALF), slice(HALF, N), slice(0, N)
+HALVES = (FIRST, SECOND)
+XT0_VECTOR = 32
+VECTOR, SCALAR = True, False
 
 
 def tile_attend_gnce_w_kernel(tc, xT, w_words, w_scales, y, wt, xm, offs, out):
@@ -37,8 +41,8 @@ def tile_attend_gnce_w_kernel(tc, xT, w_words, w_scales, y, wt, xm, offs, out):
         def sb(name, shape, dtype, tag=""):
             return keep.tile(shape, dtype, name=name, tag=tag or name, align_bytes=64)
 
-        def copy(engine, dst, src):
-            if engine:
+        def copy(on_vector, dst, src):
+            if on_vector:
                 nc.vector.tensor_copy(out=dst, in_=src)
             else:
                 nc.scalar.copy(out=dst, in_=src)
@@ -47,216 +51,202 @@ def tile_attend_gnce_w_kernel(tc, xT, w_words, w_scales, y, wt, xm, offs, out):
             return offsets[:, slots.start // BAND:slots.stop // BAND]
 
         offsets = keep.tile([P, N // BAND], U16, name="offsets")
-        xt_raw = [sb("xt_raw%d" % c, [P, PACK, KP], F32) for c in range(PASSES)]
+        xt_raw = {(0, 0): sb("xt_raw0", [P, PACK, KP], F32)}
+        for m0 in (0, P // 2):
+            xt_raw[1, m0] = sb("xt_raw1_%d" % m0, [P, PACK, KP // 2], F32)
         y_raw = [sb("y_raw%d" % c, [P, PACK, N], F32) for c in range(PASSES)]
         xm_raw = [[sb("xm_raw%d%d" % (c, h), [P, PACK, D // 2], F32) for h in range(2)] for c in range(PASSES)]
         words = sb("words", [P, T], U32)
         scales = sb("scales", [P, T], U8)
         w_rows = sb("w_rows", [P, PASSES, PACK], F32)
 
-        def load_xt(c):
-            nc.sync.dma_start(out=xt_raw[c][:], in_=xT[0][:, c * KP:(c + 1) * KP].rearrange("(p j) r -> p j r", j=PACK))
+        def load_xt(c, m0, m1):
+            rows = xT[0][:, c * KP + PACK * m0:c * KP + PACK * m1]
+            nc.sync.dma_start(out=xt_raw[c, m0][:], in_=rows.rearrange("(p j) r -> p j r", j=PACK))
 
-        def load_scales(queue):
-            nc.vector.memset(scales[:].bitcast(I32), 0)
-            for f in range(4):
-                queue.dma_start(out=scales[f:P:QUAD, :].bitcast(I32), in_=w_scales[0][f:16:4, :].bitcast(I32))
-
-        def load_words():
-            nc.sync.dma_start(out=words[:].bitcast(I32), in_=w_words[0].rearrange("p n t -> p (n t)").bitcast(I32))
-
-        def load_w(queue):
-            queue.dma_start(out=w_rows[:], in_=wt[0].rearrange("(c p t) o -> p c (t o)", p=P, t=PACK))
-
-        def load_y(c, t0, t1, slots):
+        def load_y(c, t0, t1):
             y_rows = y[0][c * KP:(c + 1) * KP, :].rearrange("(p t) i -> p t i", t=PACK)
-            nc.sync.dma_start(out=y_raw[c][:, t0:t1, slots], in_=y_rows[:, t0:t1, slots])
+            nc.sync.dma_start(out=y_raw[c][:, t0:t1, :], in_=y_rows[:, t0:t1, :])
 
         def load_xm(c, h):
             rows = xm[0][c * KP:(c + 1) * KP, h * (D // 2):(h + 1) * (D // 2)]
             nc.sync.dma_start(out=xm_raw[c][h][:], in_=rows.rearrange("(p t) d -> p t d", t=PACK))
 
-        load_xt(0)
+        load_xt(0, 0, P)
         nc.sync.dma_start(offsets[:], offs)
-        load_scales(nc.sync)
-        load_w(nc.scalar)
-        load_words()
-        load_xt(1)
-        load_y(0, 0, 2, ALL)
-        load_y(0, 2, 4, ALL)
-        load_y(1, 0, 2, ALL)
-        load_y(1, 2, 4, ALL)
-        load_xm(0, 0)
-        load_xm(1, 0)
-        load_xm(0, 1)
-        load_xm(1, 1)
+        nc.vector.memset(scales[:].bitcast(I32), 0)
+        for f in range(4):
+            nc.sync.dma_start(out=scales[f:P:QUAD, :].bitcast(I32), in_=w_scales[0][f:16:4, :].bitcast(I32))
+        nc.scalar.dma_start(out=w_rows[:], in_=wt[0].rearrange("(c p t) o -> p c (t o)", p=P, t=PACK))
+        nc.sync.dma_start(out=words[:].bitcast(I32), in_=w_words[0].rearrange("p n t -> p (n t)").bitcast(I32))
+        load_xt(1, 0, P // 2)
+        load_xt(1, P // 2, P)
+        for c in range(PASSES):
+            load_y(c, 0, 2)
+            load_y(c, 2, 4)
+        for h in range(2):
+            for c in range(PASSES):
+                load_xm(c, h)
 
-        g_codes = [sb("g_codes%d" % c, [P, HALF + N], U32) for c in range(PASSES)]
-        g_scale = [sb("g_scale%d" % c, [P, HALF + N], U8) for c in range(PASSES)]
-        windows = [sb("window%d" % k, [P, T], F32) for k in range(3)]
+        windows = [sb("window%d" % k, [P, T], F32) for k in range(DBLOCKS)]
         for window in windows:
             nc.vector.memset(window[:].bitcast(I32), 0)
-        for c in range(PASSES):
-            nc.vector.memset(g_codes[c][:, :HALF].bitcast(I32), 0)
-            nc.vector.memset(g_scale[c][:, :HALF].bitcast(I32), 0)
 
         w_scale_g = sb("w_scale_g", [P, N], U8)
         w_word_g = sb("w_word_g", [P, N], U32)
         xt_bf = [sb("xt_bf%d" % c, [P, PACK, P, PACK], BF16) for c in range(PASSES)]
         xt_codes = [sb("xt_codes%d" % c, [P, KP], U32) for c in range(PASSES)]
         xt_scale = [sb("xt_scale%d" % c, [P, KP], U8) for c in range(PASSES)]
-        sig = [[sb("sig%d%d" % (c, t), [P, N], F32) for t in range(PACK)] for c in range(PASSES)]
-        wy = [[sb("wy%d%d" % (c, t), [P, N], F32) for t in range(PACK)] for c in range(PASSES)]
-        g_rows = {(0, 0): sb("g_rows0", [P, PACK, N], BF16), (1, 0): sb("g_rows10", [P, PACK, HALF], BF16)}
-        g_packed = [[sb("g_packed%d0" % c, [P, HALF, PACK], BF16)] for c in range(PASSES)]
+        sig = [sb("sig%d" % c, [P, PACK, N], F32) for c in range(PASSES)]
+        diff = {0: sb("diff0", [P, PACK, N], F32)}
+        g_rows = {1: sb("g_rows1", [P, PACK, N], BF16)}
+        g_packed0 = sb("g_packed0", [P, N, PACK], BF16)
+        g_packed1 = [sb("g_packed1%d" % h, [P, HALF, PACK], BF16) for h in range(2)]
+        g_codes = [sb("g_codes%d" % c, [P, N], U32) for c in range(PASSES)]
+        g_scale = [sb("g_scale%d" % c, [P, N], U8) for c in range(PASSES)]
         xm_codes = sb("xm_codes", [P, DBLOCKS, PASSES, P], U32)
         xm_scale = sb("xm_scale", [P, DBLOCKS, PASSES, P], U8)
-        xm_bf = [sb("xm_bf%d" % k, [P, PASSES, P, PACK], BF16) for k in range(2)]
-        dense = {k: sb("dense%d" % k, [P, N], F32) for k in (0, 2, 3)}
+        wy = {}
+        xm_bf = {}
+        dense = {}
 
-        def gather_scales():
-            nc.vector.tensor_copy(w_scale_g[:], scales[:].indirect(entries(ALL)))
+        def packed(c, h):
+            return g_packed0[:, HALVES[h], :] if c == 0 else g_packed1[h][:]
 
-        def gather_words(slots):
-            nc.vector.tensor_copy(w_word_g[:, slots], words[:].indirect(entries(slots)))
-
-        def cast_xt(c, m0, m1, on_vector):
+        def cast_xt(c, part, m0, m1, on_vector):
             copy(on_vector, xt_bf[c][:].rearrange("p t m j -> p m j t")[:, m0:m1],
-                 xt_raw[c][:].rearrange("p j (m t) -> p m j t", t=PACK)[:, m0:m1])
+                 xt_raw[c, part][:].rearrange("p j (m t) -> p m j t", t=PACK)[:, m0 - part:m1 - part])
 
         def quant_xt(c, t0, t1):
             nc.vector.quantize_mx(out=xt_codes[c][:, t0 * P:t1 * P].bitcast(E4M3), scales=xt_scale[c][:, t0 * P:t1 * P],
                                   in_=xt_bf[c][:, t0:t1].rearrange("p t m j -> p (t m j)"))
 
-        def scores(c, t, slots, sign):
+        def scores(c, t, slots):
             acc = psum.tile([P, slots.stop - slots.start], F32, name="acc_a", tag="acc_a", bufs=4)
             cols = slice(t * P, (t + 1) * P)
             nc.tensor.matmul_mx(out=acc[:], lhsT=xt_codes[c][:, cols].bitcast(E4M3), lhsT_scale=xt_scale[c][:, cols],
                                 rhs=w_word_g[:, slots].bitcast(E4M3), rhs_scale=w_scale_g[:, slots], start=True, stop=True)
-            nc.scalar.activation(out=sig[c][t][:, slots], in_=acc[:], func=ACT.Sigmoid, scale=sign)
+            nc.scalar.activation(out=sig[c][:, t, slots], in_=acc[:], func=ACT.Sigmoid)
 
-        def weigh_y(c, t, slots, on_vector):
+        def weigh_y(c, t, on_vector):
+            dst = wy[c][:, t, :]
             if on_vector:
-                nc.vector.tensor_scalar_mul(wy[c][t][:, slots], y_raw[c][:, t, slots], w_rows[:, c, t:t + 1])
+                nc.vector.tensor_scalar_mul(dst, y_raw[c][:, t, :], w_rows[:, c, t:t + 1])
             else:
-                nc.scalar.activation(out=wy[c][t][:, slots], in_=y_raw[c][:, t, slots], func=ACT.Copy,
-                                     scale=w_rows[:, c, t:t + 1])
-
-        def rows_of_g(c, slots):
-            if c == 0:
-                return g_rows[0, 0][:, :, slots]
-            return g_rows[1, slots.start // HALF][:]
+                nc.scalar.activation(out=dst, in_=y_raw[c][:, t, :], func=ACT.Copy, scale=w_rows[:, c, t:t + 1])
 
         def grad(c, t, slots):
-            nc.vector.scalar_tensor_tensor(out=rows_of_g(c, slots)[:, t, :], in0=sig[c][t][:, slots],
-                                           scalar=w_rows[:, c, t:t + 1], in1=wy[c][t][:, slots],
+            nc.vector.scalar_tensor_tensor(out=g_rows[c][:, t, slots], in0=sig[c][:, t, slots],
+                                           scalar=w_rows[:, c, t:t + 1], in1=wy[c][:, t, slots],
                                            op0=ALU.mult, op1=ALU.subtract)
 
+        def subtract_y(c, t0, t1):
+            nc.vector.tensor_tensor(out=diff[c][:, t0:t1, :], in0=sig[c][:, t0:t1, :], in1=y_raw[c][:, t0:t1, :],
+                                    op=ALU.subtract)
+
+        def weigh_and_pack(c, h):
+            weights = w_rows[:, c, :].unsqueeze(1).unsqueeze(3).to_broadcast([P, HALF // PAIR, PACK, PAIR])
+            nc.vector.tensor_tensor(out=packed(c, h).rearrange("p (q i) t -> p q t i", i=PAIR),
+                                    in0=diff[c][:, :, HALVES[h]].rearrange("p t (q i) -> p q t i", i=PAIR),
+                                    in1=weights, op=ALU.mult)
+
         def pack_g(c, h, on_vector):
-            slots = slice(h * HALF, (h + 1) * HALF)
-            copy(on_vector, g_packed[c][h][:].rearrange("p (q i) t -> p q t i", i=RUN),
-                 rows_of_g(c, slots).rearrange("p t (q i) -> p q t i", i=RUN))
+            copy(on_vector, packed(c, h).rearrange("p (q i) t -> p q t i", i=RUN),
+                 g_rows[c][:, :, HALVES[h]].rearrange("p t (q i) -> p q t i", i=RUN))
 
         def quant_g(c, h):
-            cols = slice(HALF + h * HALF, HALF + (h + 1) * HALF)
-            nc.vector.quantize_mx(out=g_codes[c][:, cols].bitcast(E5M2), scales=g_scale[c][:, cols],
-                                  in_=g_packed[c][h][:].rearrange("p i t -> p (i t)"))
+            nc.vector.quantize_mx(out=g_codes[c][:, HALVES[h]].bitcast(E5M2), scales=g_scale[c][:, HALVES[h]],
+                                  in_=packed(c, h).rearrange("p i t -> p (i t)"))
 
         def cast_xm(k, c, on_vector):
             cols = slice((k % 2) * P, (k % 2 + 1) * P)
             copy(on_vector, xm_bf[k][:, c].rearrange("p (q i) t -> p q t i", i=RUN),
                  xm_raw[c][k // 2][:, :, cols].rearrange("p t (q i) -> p q t i", i=RUN))
 
-        def quant_xm(k, c0, c1):
-            nc.vector.quantize_mx(out=xm_codes[:, k, c0:c1].rearrange("p c m -> p (c m)").bitcast(E4M3),
-                                  scales=xm_scale[:, k, c0:c1].rearrange("p c m -> p (c m)"),
-                                  in_=xm_bf[k][:, c0:c1].rearrange("p c m t -> p (c m t)"))
+        def quant_xm(k):
+            nc.vector.quantize_mx(out=xm_codes[:, k].rearrange("p c m -> p (c m)").bitcast(E4M3),
+                                  scales=xm_scale[:, k].rearrange("p c m -> p (c m)"),
+                                  in_=xm_bf[k][:].rearrange("p c m t -> p (c m t)"))
 
-        def product(k, first_col):
-            acc = psum.tile([P, N], F32, name="acc_d", tag="acc_d", bufs=4)
-            cols = slice(first_col, first_col + N)
+        def product(k, slots):
+            acc = psum.tile([P, slots.stop - slots.start], F32, name="acc_d", tag="acc_d", bufs=4)
             for c in range(PASSES):
                 nc.tensor.matmul_mx(out=acc[:], lhsT=xm_codes[:, k, c, :].bitcast(E4M3), lhsT_scale=xm_scale[:, k, c, :],
-                                    rhs=g_codes[c][:, cols].bitcast(E5M2), rhs_scale=g_scale[c][:, cols],
+                                    rhs=g_codes[c][:, slots].bitcast(E5M2), rhs_scale=g_scale[c][:, slots],
                                     start=(c == 0), stop=(c == PASSES - 1))
             return acc
 
-        def leave(k, slots, sums):
-            nc.scalar.copy(out=dense[k][:, slots], in_=sums)
+        def leave(k, slots, on_vector):
+            width = slots.stop - slots.start
+            dense[k, slots.start] = sb("dense%d_%d" % (k, slots.start), [P, width], F32)
+            copy(on_vector, dense[k, slots.start][:], product(k, slots)[:])
 
-        def place(k, slots):
-            window = windows[k % 3]
-            nc.vector.tensor_copy(window[:].indirect(entries(slots)), dense[k][:, slots])
+        def place(k, slots, values, on_vector):
+            if on_vector:
+                nc.vector.tensor_copy(windows[k][:].indirect(entries(slots)), values)
+            else:
+                nc.scalar.activation(out=windows[k][:].indirect(entries(slots)), in_=values, func=ACT.Copy)
             if slots.stop == N:
-                nc.sync.dma_start(out=out[k * P:(k + 1) * P, :], in_=window[:])
+                nc.sync.dma_start(out=out[k * P:(k + 1) * P, :], in_=windows[k][:])
 
-        cast_xt(0, 0, 80, True)
-        cast_xt(0, 80, P, False)
-        gather_scales()
+        cast_xt(0, 0, XT0_VECTOR, P, SCALAR)
+        nc.vector.tensor_copy(w_scale_g[:], scales[:].indirect(entries(ALL)))
+        cast_xt(0, 0, 0, XT0_VECTOR, VECTOR)
         quant_xt(0, 0, 4)
-        gather_words(FIRST)
-        gather_words(SECOND)
-        scores(0, 0, FIRST, 1.0)
-        scores(0, 1, FIRST, 1.0)
-        scores(0, 0, SECOND, 1.0)
-        scores(0, 1, SECOND, 1.0)
+        for slots in HALVES:
+            nc.vector.tensor_copy(w_word_g[:, slots], words[:].indirect(entries(slots)))
+        for slots in HALVES:
+            for t in range(2):
+                scores(0, t, slots)
         for t in range(2, PACK):
-            scores(0, t, ALL, 1.0)
-        cast_xt(1, 0, P, True)
-        quant_xt(1, 0, 2)
-        quant_xt(1, 2, 4)
+            scores(0, t, ALL)
+        cast_xt(1, 0, 0, P // 2, VECTOR)
+        cast_xt(1, P // 2, P // 2, P, VECTOR)
+        quant_xt(1, 0, 4)
         for t in range(PACK):
-            weigh_y(0, t, ALL, t in (0, 2))
+            scores(1, t, ALL)
+        subtract_y(0, 0, 2)
+        subtract_y(0, 2, 4)
+        wy[1] = sb("wy1", [P, PACK, N], F32, tag="xt_codes1")
         for t in range(PACK):
-            scores(1, t, ALL, 1.0)
-        for t in range(PACK):
-            weigh_y(1, t, ALL, True)
-        for t in range(PACK):
-            grad(0, t, ALL)
+            weigh_y(1, t, SCALAR)
+        xm_bf[0] = sb("xm_bf0", [P, PASSES, P, PACK], BF16, tag="xt_scale1")
+        for c in range(PASSES):
+            cast_xm(0, c, SCALAR)
+        weigh_and_pack(0, 0)
+        weigh_and_pack(0, 1)
         for t in range(PACK):
             grad(1, t, FIRST)
-        pack_g(0, 0, False)
-        cast_xm(0, 0, False)
-        cast_xm(0, 1, True)
-        pack_g(1, 0, True)
+        pack_g(1, 0, SCALAR)
         quant_g(0, 0)
-        quant_xm(0, 0, 1)
-        quant_xm(0, 1, 2)
-        quant_g(1, 0)
-        early0 = product(0, 0)
-        g_rows[1, 1] = sb("g_rows11", [P, PACK, HALF], BF16, tag="xm_bf0")
+        quant_g(0, 1)
         for t in range(PACK):
             grad(1, t, SECOND)
-        for c in range(PASSES):
-            cast_xm(1, c, False)
-        quant_xm(1, 0, 2)
-        g_packed[0].append(sb("g_packed01", [P, HALF, PACK], BF16, tag="xm_raw10"))
-        g_packed[1].append(sb("g_packed11", [P, HALF, PACK], BF16))
-        pack_g(0, 1, False)
-        leave(0, FIRST, early0[:, HALF:])
-        pack_g(1, 1, False)
-        quant_g(0, 1)
+        quant_xm(0)
+        quant_g(1, 0)
+        leave(0, FIRST, SCALAR)
+        place(0, FIRST, dense[0, 0][:], SCALAR)
+        pack_g(1, 1, VECTOR)
+        xm_bf[1] = sb("xm_bf1", [P, PASSES, P, PACK], BF16, tag="g_packed10")
+        cast_xm(1, 0, VECTOR)
         quant_g(1, 1)
-        early1 = product(1, 0)
-        dense[1] = sb("dense1", [P, N], F32, tag="xm_bf0")
-        leave(1, FIRST, early1[:, HALF:])
-        full0 = product(0, HALF)
-        place(0, FIRST)
-        xm_late = sb("xm_late", [P, 2, PASSES, P, PACK], BF16, tag="g_packed11")
-        xm_bf.extend(xm_late[:, k] for k in range(2))
-        for c in range(PASSES):
-            cast_xm(2, c, False)
-        quant_xm(2, 0, 2)
-        leave(0, SECOND, full0[:, SECOND])
-        full1 = product(1, HALF)
-        for c in range(PASSES):
-            cast_xm(3, c, False)
-        quant_xm(3, 0, 2)
-        leave(1, SECOND, full1[:, SECOND])
-        place(1, FIRST)
-        for k in range(2, DBLOCKS):
-            leave(k, ALL, product(k, HALF)[:])
-        place(0, SECOND)
-        place(1, SECOND)
-        for k in range(2, DBLOCKS):
-            place(k, ALL)
+        cast_xm(1, 1, VECTOR)
+        xm_bf[2] = sb("xm_bf2", [P, PASSES, P, PACK], BF16, tag="g_packed11")
+        cast_xm(2, 0, VECTOR)
+        quant_xm(1)
+        leave(0, SECOND, VECTOR)
+        place(0, SECOND, dense[0, HALF][:], VECTOR)
+        for slots in HALVES:
+            leave(1, slots, SCALAR)
+            place(1, slots, dense[1, slots.start][:], SCALAR)
+        xm_bf[3] = sb("xm_bf3", [P, PASSES, P, PACK], BF16, tag="dense0_%d" % HALF)
+        cast_xm(2, 1, VECTOR)
+        cast_xm(3, 0, VECTOR)
+        quant_xm(2)
+        cast_xm(3, 1, VECTOR)
+        quant_xm(3)
+        leave(2, ALL, VECTOR)
+        place(2, ALL, dense[2, 0][:], VECTOR)
+        leave(3, ALL, SCALAR)
+        for slots in HALVES:
+            place(3, slots, dense[3, 0][:, slots], SCALAR)

@@ -55,7 +55,7 @@ def tile_attend_gnce_w_kernel(tc, xT, w_words, w_scales, y, wt, xm, offs, out):
         for m0 in (0, P // 2):
             xt_raw[1, m0] = sb("xt_raw1_%d" % m0, [P, PACK, KP // 2], F32)
         y_raw = [sb("y_raw%d" % c, [P, PACK, N], F32) for c in range(PASSES)]
-        xm_raw = [[sb("xm_raw%d%d" % (c, h), [P, PACK, D // 2], F32) for h in range(2)] for c in range(PASSES)]
+        xm_raw = [sb("xm_raw%d" % h, [P, PASSES, PACK, D // 2], F32) for h in range(2)]
         words = sb("words", [P, T], U32)
         scales = sb("scales", [P, T], U8)
         w_rows = sb("w_rows", [P, PASSES, PACK], F32)
@@ -70,7 +70,7 @@ def tile_attend_gnce_w_kernel(tc, xT, w_words, w_scales, y, wt, xm, offs, out):
 
         def load_xm(c, h):
             rows = xm[0][c * KP:(c + 1) * KP, h * (D // 2):(h + 1) * (D // 2)]
-            nc.sync.dma_start(out=xm_raw[c][h][:], in_=rows.rearrange("(p t) d -> p t d", t=PACK))
+            nc.sync.dma_start(out=xm_raw[h][:, c], in_=rows.rearrange("(p t) d -> p t d", t=PACK))
 
         load_xt(0, 0, P)
         nc.sync.dma_start(offsets[:], offs)
@@ -88,7 +88,7 @@ def tile_attend_gnce_w_kernel(tc, xT, w_words, w_scales, y, wt, xm, offs, out):
             for c in range(PASSES):
                 load_xm(c, h)
 
-        windows = [sb("window%d" % k, [P, T], F32) for k in range(DBLOCKS)]
+        windows = [sb("window%d" % k, [P, T], F32) for k in range(2)]
         for window in windows:
             nc.vector.memset(window[:].bitcast(I32), 0)
 
@@ -98,20 +98,24 @@ def tile_attend_gnce_w_kernel(tc, xT, w_words, w_scales, y, wt, xm, offs, out):
         xt_codes = [sb("xt_codes%d" % c, [P, KP], U32) for c in range(PASSES)]
         xt_scale = [sb("xt_scale%d" % c, [P, KP], U8) for c in range(PASSES)]
         sig = [sb("sig%d" % c, [P, PACK, N], F32) for c in range(PASSES)]
-        diff = {0: sb("diff0", [P, PACK, N], F32)}
-        g_rows = {1: sb("g_rows1", [P, PACK, N], BF16)}
-        g_packed0 = sb("g_packed0", [P, N, PACK], BF16)
-        g_packed1 = [sb("g_packed1%d" % h, [P, HALF, PACK], BF16) for h in range(2)]
+        diff = {1: sb("diff1", [P, PACK, N], F32)}
+        g_rows = {0: sb("g_rows0", [P, PACK, N], BF16)}
+        g_packed = [[sb("g_packed0%d" % h, [P, HALF, PACK], BF16) for h in range(2)],
+                    [sb("g_packed10", [P, HALF, PACK], BF16)]]
         g_codes = [sb("g_codes%d" % c, [P, N], U32) for c in range(PASSES)]
         g_scale = [sb("g_scale%d" % c, [P, N], U8) for c in range(PASSES)]
-        xm_codes = sb("xm_codes", [P, DBLOCKS, PASSES, P], U32)
-        xm_scale = sb("xm_scale", [P, DBLOCKS, PASSES, P], U8)
+        xm_codes = {k: sb("xm_codes%d" % k, [P, PASSES, P], U32) for k in (0, 3)}
+        xm_scale = [sb("xm_scale%d" % k, [P, PASSES, P], U8) for k in range(DBLOCKS)]
         wy = {}
         xm_bf = {}
         dense = {}
 
         def packed(c, h):
-            return g_packed0[:, HALVES[h], :] if c == 0 else g_packed1[h][:]
+            return g_packed[c][h][:]
+
+        def clear_on_gpsimd(window):
+            for part in range(2):
+                nc.gpsimd.memset(window[:, part * T // 2:(part + 1) * T // 2].bitcast(I32), 0)
 
         def cast_xt(c, part, m0, m1, on_vector):
             copy(on_vector, xt_bf[c][:].rearrange("p t m j -> p m j t")[:, m0:m1],
@@ -129,7 +133,7 @@ def tile_attend_gnce_w_kernel(tc, xT, w_words, w_scales, y, wt, xm, offs, out):
             nc.scalar.activation(out=sig[c][:, t, slots], in_=acc[:], func=ACT.Sigmoid)
 
         def weigh_y(c, t, on_vector):
-            dst = wy[c][:, t, :]
+            dst = wy[c, t][:]
             if on_vector:
                 nc.vector.tensor_scalar_mul(dst, y_raw[c][:, t, :], w_rows[:, c, t:t + 1])
             else:
@@ -137,7 +141,7 @@ def tile_attend_gnce_w_kernel(tc, xT, w_words, w_scales, y, wt, xm, offs, out):
 
         def grad(c, t, slots):
             nc.vector.scalar_tensor_tensor(out=g_rows[c][:, t, slots], in0=sig[c][:, t, slots],
-                                           scalar=w_rows[:, c, t:t + 1], in1=wy[c][:, t, slots],
+                                           scalar=w_rows[:, c, t:t + 1], in1=wy[c, t][:, slots],
                                            op0=ALU.mult, op1=ALU.subtract)
 
         def subtract_y(c, t0, t1):
@@ -158,20 +162,25 @@ def tile_attend_gnce_w_kernel(tc, xT, w_words, w_scales, y, wt, xm, offs, out):
             nc.vector.quantize_mx(out=g_codes[c][:, HALVES[h]].bitcast(E5M2), scales=g_scale[c][:, HALVES[h]],
                                   in_=packed(c, h).rearrange("p i t -> p (i t)"))
 
-        def cast_xm(k, c, on_vector):
+        def cast_xm(k, c0, c1, on_vector):
             cols = slice((k % 2) * P, (k % 2 + 1) * P)
-            copy(on_vector, xm_bf[k][:, c].rearrange("p (q i) t -> p q t i", i=RUN),
-                 xm_raw[c][k // 2][:, :, cols].rearrange("p t (q i) -> p q t i", i=RUN))
+            copy(on_vector, xm_bf[k][:, c0:c1].rearrange("p c (q i) t -> p c q t i", i=RUN),
+                 xm_raw[k // 2][:, c0:c1, :, cols].rearrange("p c t (q i) -> p c q t i", i=RUN))
+
+        def cast_xm_on_gpsimd(k, c):
+            cols = slice((k % 2) * P, (k % 2 + 1) * P)
+            nc.gpsimd.tensor_scalar(out=xm_bf[k][:, c], in0=xm_raw[k // 2][:, c, :, cols].rearrange("p t m -> p m t"),
+                                    scalar1=1.0, scalar2=0.0, op0=ALU.mult, op1=ALU.add)
 
         def quant_xm(k):
-            nc.vector.quantize_mx(out=xm_codes[:, k].rearrange("p c m -> p (c m)").bitcast(E4M3),
-                                  scales=xm_scale[:, k].rearrange("p c m -> p (c m)"),
-                                  in_=xm_bf[k][:].rearrange("p c m t -> p (c m t)"))
+            nc.vector.quantize_mx(out=xm_codes[k][:].rearrange("p c m -> p (c m)").bitcast(E4M3),
+                                  scales=xm_scale[k][:].rearrange("p c m -> p (c m)"),
+                                  in_=xm_bf[k][:, :].rearrange("p c m t -> p (c m t)"))
 
         def product(k, slots):
             acc = psum.tile([P, slots.stop - slots.start], F32, name="acc_d", tag="acc_d", bufs=4)
             for c in range(PASSES):
-                nc.tensor.matmul_mx(out=acc[:], lhsT=xm_codes[:, k, c, :].bitcast(E4M3), lhsT_scale=xm_scale[:, k, c, :],
+                nc.tensor.matmul_mx(out=acc[:], lhsT=xm_codes[k][:, c, :].bitcast(E4M3), lhsT_scale=xm_scale[k][:, c, :],
                                     rhs=g_codes[c][:, slots].bitcast(E5M2), rhs_scale=g_scale[c][:, slots],
                                     start=(c == 0), stop=(c == PASSES - 1))
             return acc
@@ -203,50 +212,60 @@ def tile_attend_gnce_w_kernel(tc, xT, w_words, w_scales, y, wt, xm, offs, out):
         cast_xt(1, 0, 0, P // 2, VECTOR)
         cast_xt(1, P // 2, P // 2, P, VECTOR)
         quant_xt(1, 0, 4)
-        for t in range(PACK):
+        windows.append(sb("window2", [P, T], F32, tag="xt_bf1"))
+        clear_on_gpsimd(windows[2])
+        wy[0, 0] = sb("wy00", [P, N], F32)
+        wy[0, 1] = sb("wy01", [P, N], F32, tag="xt_codes0")
+        wy[0, 2] = sb("wy02", [P, N], F32)
+        wy[0, 3] = sb("wy03", [P, N], F32, tag="xt_scale0")
+        weigh_y(0, 1, SCALAR)
+        for t in range(2):
             scores(1, t, ALL)
-        subtract_y(0, 0, 2)
-        subtract_y(0, 2, 4)
-        wy[1] = sb("wy1", [P, PACK, N], F32, tag="xt_codes1")
+        weigh_y(0, 3, SCALAR)
+        for t in range(2, PACK):
+            scores(1, t, ALL)
         for t in range(PACK):
-            weigh_y(1, t, SCALAR)
-        xm_bf[0] = sb("xm_bf0", [P, PASSES, P, PACK], BF16, tag="xt_scale1")
-        for c in range(PASSES):
-            cast_xm(0, c, SCALAR)
-        weigh_and_pack(0, 0)
-        weigh_and_pack(0, 1)
-        for t in range(PACK):
-            grad(1, t, FIRST)
-        pack_g(1, 0, SCALAR)
+            if t % 2 == 0:
+                weigh_y(0, t, VECTOR)
+            grad(0, t, ALL)
+        windows.append(sb("window3", [P, T], F32, tag="y_raw0"))
+        clear_on_gpsimd(windows[3])
+        subtract_y(1, 0, 2)
+        subtract_y(1, 2, 4)
+        pack_g(0, 0, SCALAR)
+        pack_g(0, 1, SCALAR)
+        xm_bf[0] = sb("xm_bf0", [P, PASSES, P, PACK], BF16, tag="xt_scale0")
+        xm_bf[1] = sb("xm_bf1", [P, PASSES, P, PACK], BF16, tag="sig0")
+        for k in range(2):
+            cast_xm(k, 0, PASSES, SCALAR)
         quant_g(0, 0)
-        quant_g(0, 1)
-        for t in range(PACK):
-            grad(1, t, SECOND)
+        weigh_and_pack(1, 0)
         quant_xm(0)
         quant_g(1, 0)
         leave(0, FIRST, SCALAR)
         place(0, FIRST, dense[0, 0][:], SCALAR)
-        pack_g(1, 1, VECTOR)
-        xm_bf[1] = sb("xm_bf1", [P, PASSES, P, PACK], BF16, tag="g_packed10")
-        cast_xm(1, 0, VECTOR)
+        g_packed[1].append(sb("g_packed11", [P, HALF, PACK], BF16, tag="xt_scale0"))
+        weigh_and_pack(1, 1)
+        quant_g(0, 1)
         quant_g(1, 1)
-        cast_xm(1, 1, VECTOR)
-        xm_bf[2] = sb("xm_bf2", [P, PASSES, P, PACK], BF16, tag="g_packed11")
-        cast_xm(2, 0, VECTOR)
+        xm_codes[1] = sb("xm_codes1", [P, PASSES, P], U32, tag="xt_scale0")
         quant_xm(1)
+        xm_late = sb("xm_late", [P, 2, PASSES, P, PACK], BF16, tag="sig0")
+        xm_bf[2] = xm_late[:, 0]
+        xm_bf[3] = xm_late[:, 1]
+        cast_xm_on_gpsimd(2, 0)
+        cast_xm_on_gpsimd(2, 1)
+        cast_xm_on_gpsimd(3, 0)
         leave(0, SECOND, VECTOR)
         place(0, SECOND, dense[0, HALF][:], VECTOR)
         for slots in HALVES:
             leave(1, slots, SCALAR)
             place(1, slots, dense[1, slots.start][:], SCALAR)
-        xm_bf[3] = sb("xm_bf3", [P, PASSES, P, PACK], BF16, tag="dense0_%d" % HALF)
-        cast_xm(2, 1, VECTOR)
-        cast_xm(3, 0, VECTOR)
+        xm_codes[2] = sb("xm_codes2", [P, PASSES, P], U32, tag="dense0_%d" % HALF)
         quant_xm(2)
-        cast_xm(3, 1, VECTOR)
+        cast_xm(3, 1, 2, VECTOR)
         quant_xm(3)
-        leave(2, ALL, VECTOR)
-        place(2, ALL, dense[2, 0][:], VECTOR)
-        leave(3, ALL, SCALAR)
-        for slots in HALVES:
-            place(3, slots, dense[3, 0][:, slots], SCALAR)
+        for k, on_vector in ((2, VECTOR), (3, SCALAR)):
+            for slots in HALVES:
+                leave(k, slots, on_vector)
+                place(k, slots, dense[k, slots.start][:], on_vector)

@@ -24,7 +24,6 @@ DBLOCKS = D // P
 BAND = 16
 QUAD = 32
 RUN = 4
-PAIR = 2
 HALF = N // 2
 FIRST, SECOND, ALL = slice(0, HALF), slice(HALF, N), slice(0, N)
 HALVES = (FIRST, SECOND)
@@ -99,12 +98,12 @@ def tile_attend_gnce_w_kernel(tc, xT, w_words, w_scales, y, wt, xm, offs, out):
         xt_scale = [sb("xt_scale%d" % c, [P, KP], U8) for c in range(PASSES)]
         sig = [sb("sig%d" % c, [P, PACK, N], F32) for c in range(PASSES)]
         diff = {1: sb("diff1", [P, PACK, N], F32)}
-        g_rows = {0: sb("g_rows0", [P, PACK, N], BF16)}
+        g_rows = [sb("g_rows%d" % c, [P, PACK, N], BF16) for c in range(PASSES)]
         g_packed = [[sb("g_packed0%d" % h, [P, HALF, PACK], BF16) for h in range(2)],
                     [sb("g_packed10", [P, HALF, PACK], BF16)]]
         g_codes = [sb("g_codes%d" % c, [P, N], U32) for c in range(PASSES)]
         g_scale = [sb("g_scale%d" % c, [P, N], U8) for c in range(PASSES)]
-        xm_codes = {k: sb("xm_codes%d" % k, [P, PASSES, P], U32) for k in (0, 3)}
+        xm_codes = {k: sb("xm_codes%d" % k, [P, PASSES, P], U32) for k in (0, 2, 3)}
         xm_scale = [sb("xm_scale%d" % k, [P, PASSES, P], U8) for k in range(DBLOCKS)]
         wy = {}
         xm_bf = {}
@@ -149,10 +148,9 @@ def tile_attend_gnce_w_kernel(tc, xT, w_words, w_scales, y, wt, xm, offs, out):
                                     op=ALU.subtract)
 
         def weigh_and_pack(c, h):
-            weights = w_rows[:, c, :].unsqueeze(1).unsqueeze(3).to_broadcast([P, HALF // PAIR, PACK, PAIR])
-            nc.vector.tensor_tensor(out=packed(c, h).rearrange("p (q i) t -> p q t i", i=PAIR),
-                                    in0=diff[c][:, :, HALVES[h]].rearrange("p t (q i) -> p q t i", i=PAIR),
-                                    in1=weights, op=ALU.mult)
+            for t in range(PACK):
+                nc.vector.tensor_scalar_mul(g_rows[c][:, t, HALVES[h]], diff[c][:, t, HALVES[h]], w_rows[:, c, t:t + 1])
+            pack_g(c, h, VECTOR)
 
         def pack_g(c, h, on_vector):
             copy(on_vector, packed(c, h).rearrange("p (q i) t -> p q t i", i=RUN),
@@ -166,11 +164,6 @@ def tile_attend_gnce_w_kernel(tc, xT, w_words, w_scales, y, wt, xm, offs, out):
             cols = slice((k % 2) * P, (k % 2 + 1) * P)
             copy(on_vector, xm_bf[k][:, c0:c1].rearrange("p c (q i) t -> p c q t i", i=RUN),
                  xm_raw[k // 2][:, c0:c1, :, cols].rearrange("p c t (q i) -> p c q t i", i=RUN))
-
-        def cast_xm_on_gpsimd(k, c):
-            cols = slice((k % 2) * P, (k % 2 + 1) * P)
-            nc.gpsimd.tensor_scalar(out=xm_bf[k][:, c], in0=xm_raw[k // 2][:, c, :, cols].rearrange("p t m -> p m t"),
-                                    scalar1=1.0, scalar2=0.0, op0=ALU.mult, op1=ALU.add)
 
         def quant_xm(k):
             nc.vector.quantize_mx(out=xm_codes[k][:].rearrange("p c m -> p (c m)").bitcast(E4M3),
@@ -212,8 +205,6 @@ def tile_attend_gnce_w_kernel(tc, xT, w_words, w_scales, y, wt, xm, offs, out):
         cast_xt(1, 0, 0, P // 2, VECTOR)
         cast_xt(1, P // 2, P // 2, P, VECTOR)
         quant_xt(1, 0, 4)
-        windows.append(sb("window2", [P, T], F32, tag="xt_bf1"))
-        clear_on_gpsimd(windows[2])
         wy[0, 0] = sb("wy00", [P, N], F32)
         wy[0, 1] = sb("wy01", [P, N], F32, tag="xt_codes0")
         wy[0, 2] = sb("wy02", [P, N], F32)
@@ -228,8 +219,8 @@ def tile_attend_gnce_w_kernel(tc, xT, w_words, w_scales, y, wt, xm, offs, out):
             if t % 2 == 0:
                 weigh_y(0, t, VECTOR)
             grad(0, t, ALL)
-        windows.append(sb("window3", [P, T], F32, tag="y_raw0"))
-        clear_on_gpsimd(windows[3])
+        windows.append(sb("window2", [P, T], F32, tag="y_raw0"))
+        clear_on_gpsimd(windows[2])
         subtract_y(1, 0, 2)
         subtract_y(1, 2, 4)
         pack_g(0, 0, SCALAR)
@@ -250,18 +241,18 @@ def tile_attend_gnce_w_kernel(tc, xT, w_words, w_scales, y, wt, xm, offs, out):
         quant_g(1, 1)
         xm_codes[1] = sb("xm_codes1", [P, PASSES, P], U32, tag="xt_scale0")
         quant_xm(1)
-        xm_late = sb("xm_late", [P, 2, PASSES, P, PACK], BF16, tag="sig0")
-        xm_bf[2] = xm_late[:, 0]
-        xm_bf[3] = xm_late[:, 1]
-        cast_xm_on_gpsimd(2, 0)
-        cast_xm_on_gpsimd(2, 1)
-        cast_xm_on_gpsimd(3, 0)
+        windows.append(sb("window3", [P, T], F32, tag="sig0"))
+        clear_on_gpsimd(windows[3])
         leave(0, SECOND, VECTOR)
         place(0, SECOND, dense[0, HALF][:], VECTOR)
         for slots in HALVES:
             leave(1, slots, SCALAR)
             place(1, slots, dense[1, slots.start][:], SCALAR)
-        xm_codes[2] = sb("xm_codes2", [P, PASSES, P], U32, tag="dense0_%d" % HALF)
+        xm_late = sb("xm_late", [P, 2, PASSES, P, PACK], BF16, tag="dense0_%d" % HALF)
+        xm_bf[2] = xm_late[:, 0]
+        xm_bf[3] = xm_late[:, 1]
+        cast_xm(2, 0, 2, VECTOR)
+        cast_xm(3, 0, 1, VECTOR)
         quant_xm(2)
         cast_xm(3, 1, 2, VECTOR)
         quant_xm(3)

@@ -35,10 +35,14 @@ def tile_attend_gnce_w_kernel(tc, xT, w_words, w_scales, y, wt, xm, offs, out):
     nc = tc.nc
     with ExitStack() as ctx:
         keep = ctx.enter_context(tc.tile_pool(name="keep", bufs=1))
+        shared = ctx.enter_context(tc.tile_pool(name="shared", bufs=1))
         psum = ctx.enter_context(tc.psum_pool(name="psum", bufs=2))
 
         def sb(name, shape, dtype, tag=""):
             return keep.tile(shape, dtype, name=name, tag=tag or name, align_bytes=64)
+
+        def laid(name, shape, dtype, at):
+            return shared.tile(shape, dtype, name=name, tag=name, align_bytes=64, offset=at)
 
         def copy(on_vector, dst, src):
             if on_vector:
@@ -50,10 +54,8 @@ def tile_attend_gnce_w_kernel(tc, xT, w_words, w_scales, y, wt, xm, offs, out):
             return offsets[:, slots.start // BAND:slots.stop // BAND]
 
         offsets = keep.tile([P, N // BAND], U16, name="offsets")
-        xt_raw = {(0, 0): sb("xt_raw0", [P, PACK, KP], F32)}
-        for m0 in (0, P // 2):
-            xt_raw[1, m0] = sb("xt_raw1_%d" % m0, [P, PACK, KP // 2], F32)
-        y_raw = [sb("y_raw%d" % c, [P, PACK, N], F32) for c in range(PASSES)]
+        xt_raw = {(c, 0): sb("xt_raw%d" % c, [P, PACK, KP], F32) for c in range(PASSES)}
+        y_raw = [[sb("y_raw%d%d" % (c, u), [P, 2, N], F32) for u in range(2)] for c in range(PASSES)]
         xm_raw = [sb("xm_raw%d" % h, [P, PASSES, PACK, D // 2], F32) for h in range(2)]
         words = sb("words", [P, T], U32)
         scales = sb("scales", [P, T], U8)
@@ -63,9 +65,9 @@ def tile_attend_gnce_w_kernel(tc, xT, w_words, w_scales, y, wt, xm, offs, out):
             rows = xT[0][:, c * KP + PACK * m0:c * KP + PACK * m1]
             nc.sync.dma_start(out=xt_raw[c, m0][:], in_=rows.rearrange("(p j) r -> p j r", j=PACK))
 
-        def load_y(c, t0, t1):
+        def load_y(c, u):
             y_rows = y[0][c * KP:(c + 1) * KP, :].rearrange("(p t) i -> p t i", t=PACK)
-            nc.sync.dma_start(out=y_raw[c][:, t0:t1, :], in_=y_rows[:, t0:t1, :])
+            nc.sync.dma_start(out=y_raw[c][u][:], in_=y_rows[:, 2 * u:2 * u + 2, :])
 
         def load_xm(c, h):
             rows = xm[0][c * KP:(c + 1) * KP, h * (D // 2):(h + 1) * (D // 2)]
@@ -78,11 +80,10 @@ def tile_attend_gnce_w_kernel(tc, xT, w_words, w_scales, y, wt, xm, offs, out):
             nc.sync.dma_start(out=scales[f:P:QUAD, :].bitcast(I32), in_=w_scales[0][f:16:4, :].bitcast(I32))
         nc.scalar.dma_start(out=w_rows[:], in_=wt[0].rearrange("(c p t) o -> p c (t o)", p=P, t=PACK))
         nc.sync.dma_start(out=words[:].bitcast(I32), in_=w_words[0].rearrange("p n t -> p (n t)").bitcast(I32))
-        load_xt(1, 0, P // 2)
-        load_xt(1, P // 2, P)
+        load_xt(1, 0, P)
         for c in range(PASSES):
-            load_y(c, 0, 2)
-            load_y(c, 2, 4)
+            for u in range(2):
+                load_y(c, u)
         for h in range(2):
             for c in range(PASSES):
                 load_xm(c, h)
@@ -96,7 +97,7 @@ def tile_attend_gnce_w_kernel(tc, xT, w_words, w_scales, y, wt, xm, offs, out):
         xt_bf = [sb("xt_bf%d" % c, [P, PACK, P, PACK], BF16) for c in range(PASSES)]
         xt_codes = [sb("xt_codes%d" % c, [P, KP], U32) for c in range(PASSES)]
         xt_scale = [sb("xt_scale%d" % c, [P, KP], U8) for c in range(PASSES)]
-        sig = [sb("sig%d" % c, [P, PACK, N], F32) for c in range(PASSES)]
+        sig = {(c, u): sb("sig%d%d" % (c, u), [P, 2, N], F32) for c, u in ((0, 0), (0, 1), (1, 0))}
         diff = {1: sb("diff1", [P, PACK, N], F32)}
         g_rows = [sb("g_rows%d" % c, [P, PACK, N], BF16) for c in range(PASSES)]
         g_packed = [[sb("g_packed0%d" % h, [P, HALF, PACK], BF16) for h in range(2)],
@@ -129,28 +130,27 @@ def tile_attend_gnce_w_kernel(tc, xT, w_words, w_scales, y, wt, xm, offs, out):
             cols = slice(t * P, (t + 1) * P)
             nc.tensor.matmul_mx(out=acc[:], lhsT=xt_codes[c][:, cols].bitcast(E4M3), lhsT_scale=xt_scale[c][:, cols],
                                 rhs=w_word_g[:, slots].bitcast(E4M3), rhs_scale=w_scale_g[:, slots], start=True, stop=True)
-            nc.scalar.activation(out=sig[c][:, t, slots], in_=acc[:], func=ACT.Sigmoid)
+            nc.scalar.activation(out=sig[c, t // 2][:, t % 2, slots], in_=acc[:], func=ACT.Sigmoid)
 
         def weigh_y(c, t, on_vector):
             dst = wy[c, t][:]
             if on_vector:
-                nc.vector.tensor_scalar_mul(dst, y_raw[c][:, t, :], w_rows[:, c, t:t + 1])
+                nc.vector.tensor_scalar_mul(dst, y_raw[c][t // 2][:, t % 2, :], w_rows[:, c, t:t + 1])
             else:
-                nc.scalar.activation(out=dst, in_=y_raw[c][:, t, :], func=ACT.Copy, scale=w_rows[:, c, t:t + 1])
+                nc.scalar.activation(out=dst, in_=y_raw[c][t // 2][:, t % 2, :], func=ACT.Copy, scale=w_rows[:, c, t:t + 1])
 
         def grad(c, t, slots):
-            nc.vector.scalar_tensor_tensor(out=g_rows[c][:, t, slots], in0=sig[c][:, t, slots],
+            nc.vector.scalar_tensor_tensor(out=g_rows[c][:, t, slots], in0=sig[c, t // 2][:, t % 2, slots],
                                            scalar=w_rows[:, c, t:t + 1], in1=wy[c, t][:, slots],
                                            op0=ALU.mult, op1=ALU.subtract)
 
-        def subtract_y(c, t0, t1):
-            nc.vector.tensor_tensor(out=diff[c][:, t0:t1, :], in0=sig[c][:, t0:t1, :], in1=y_raw[c][:, t0:t1, :],
+        def subtract_y(c, u):
+            nc.vector.tensor_tensor(out=diff[c][:, 2 * u:2 * u + 2, :], in0=sig[c, u][:], in1=y_raw[c][u][:],
                                     op=ALU.subtract)
 
-        def weigh_and_pack(c, h):
+        def weigh_diff(c, h):
             for t in range(PACK):
                 nc.vector.tensor_scalar_mul(g_rows[c][:, t, HALVES[h]], diff[c][:, t, HALVES[h]], w_rows[:, c, t:t + 1])
-            pack_g(c, h, VECTOR)
 
         def pack_g(c, h, on_vector):
             copy(on_vector, packed(c, h).rearrange("p (q i) t -> p q t i", i=RUN),
@@ -202,61 +202,69 @@ def tile_attend_gnce_w_kernel(tc, xT, w_words, w_scales, y, wt, xm, offs, out):
                 scores(0, t, slots)
         for t in range(2, PACK):
             scores(0, t, ALL)
-        cast_xt(1, 0, 0, P // 2, VECTOR)
-        cast_xt(1, P // 2, P // 2, P, VECTOR)
+        cast_xt(1, 0, 0, P, VECTOR)
         quant_xt(1, 0, 4)
         wy[0, 0] = sb("wy00", [P, N], F32)
         wy[0, 1] = sb("wy01", [P, N], F32, tag="xt_codes0")
-        wy[0, 2] = sb("wy02", [P, N], F32)
-        wy[0, 3] = sb("wy03", [P, N], F32, tag="xt_scale0")
+        wy[0, 2] = sb("wy02", [P, N], F32, tag="xt_scale0")
+        wy[0, 3] = sb("wy03", [P, N], F32)
         weigh_y(0, 1, SCALAR)
         for t in range(2):
             scores(1, t, ALL)
-        weigh_y(0, 3, SCALAR)
+        weigh_y(0, 2, SCALAR)
+        weigh_y(0, 0, VECTOR)
+        grad(0, 0, ALL)
+        grad(0, 1, ALL)
+        weigh_y(0, 3, VECTOR)
+        sig[1, 1] = sb("sig11", [P, 2, N], F32, tag="y_raw01")
         for t in range(2, PACK):
             scores(1, t, ALL)
-        for t in range(PACK):
-            if t % 2 == 0:
-                weigh_y(0, t, VECTOR)
-            grad(0, t, ALL)
-        windows.append(sb("window2", [P, T], F32, tag="y_raw0"))
+        grad(0, 3, ALL)
+        windows.append(sb("window2", [P, T], F32, tag="wy03"))
         clear_on_gpsimd(windows[2])
-        subtract_y(1, 0, 2)
-        subtract_y(1, 2, 4)
+        grad(0, 2, ALL)
+        subtract_y(1, 0)
+        subtract_y(1, 1)
         pack_g(0, 0, SCALAR)
         pack_g(0, 1, SCALAR)
         xm_bf[0] = sb("xm_bf0", [P, PASSES, P, PACK], BF16, tag="xt_scale0")
-        xm_bf[1] = sb("xm_bf1", [P, PASSES, P, PACK], BF16, tag="sig0")
+        xm_bf[1] = sb("xm_bf1", [P, PASSES, P, PACK], BF16, tag="sig01")
         for k in range(2):
             cast_xm(k, 0, PASSES, SCALAR)
+        weigh_diff(1, 0)
         quant_g(0, 0)
-        weigh_and_pack(1, 0)
+        pack_g(1, 0, VECTOR)
         quant_xm(0)
         quant_g(1, 0)
         leave(0, FIRST, SCALAR)
         place(0, FIRST, dense[0, 0][:], SCALAR)
-        g_packed[1].append(sb("g_packed11", [P, HALF, PACK], BF16, tag="xt_scale0"))
-        weigh_and_pack(1, 1)
+        g_rows_late = sb("g_rows_late", [P, PACK, HALF], BF16, tag="xt_scale0")
+        for t in range(PACK):
+            nc.vector.tensor_scalar_mul(g_rows_late[:, t, :], diff[1][:, t, SECOND], w_rows[:, 1, t:t + 1])
         quant_g(0, 1)
-        quant_g(1, 1)
+        g_packed[1].append(laid("g_packed11", [P, HALF, PACK], BF16, 1024))
+        nc.vector.tensor_copy(out=packed(1, 1).rearrange("p (q i) t -> p q t i", i=RUN),
+                              in_=g_rows_late[:].rearrange("p t (q i) -> p q t i", i=RUN))
         xm_codes[1] = sb("xm_codes1", [P, PASSES, P], U32, tag="xt_scale0")
         quant_xm(1)
-        windows.append(sb("window3", [P, T], F32, tag="sig0"))
-        clear_on_gpsimd(windows[3])
+        quant_g(1, 1)
+        xm_bf[2] = laid("xm_bf2", [P, PASSES, P, PACK], BF16, 1024)
+        cast_xm(2, 0, PASSES, VECTOR)
         leave(0, SECOND, VECTOR)
+        quant_xm(2)
+        windows.append(laid("window3", [P, T], F32, 2048))
+        clear_on_gpsimd(windows[3])
         place(0, SECOND, dense[0, HALF][:], VECTOR)
         for slots in HALVES:
             leave(1, slots, SCALAR)
             place(1, slots, dense[1, slots.start][:], SCALAR)
-        xm_late = sb("xm_late", [P, 2, PASSES, P, PACK], BF16, tag="dense0_%d" % HALF)
-        xm_bf[2] = xm_late[:, 0]
-        xm_bf[3] = xm_late[:, 1]
-        cast_xm(2, 0, 2, VECTOR)
-        cast_xm(3, 0, 1, VECTOR)
-        quant_xm(2)
-        cast_xm(3, 1, 2, VECTOR)
+        xm_bf[3] = laid("xm_bf3", [P, PASSES, P, PACK], BF16, 0)
+        cast_xm(3, 0, PASSES, VECTOR)
+        leave(2, FIRST, VECTOR)
         quant_xm(3)
-        for k, on_vector in ((2, VECTOR), (3, SCALAR)):
-            for slots in HALVES:
-                leave(k, slots, on_vector)
-                place(k, slots, dense[k, slots.start][:], on_vector)
+        leave(2, SECOND, SCALAR)
+        for slots in HALVES:
+            place(2, slots, dense[2, slots.start][:], VECTOR)
+        for slots in HALVES:
+            leave(3, slots, SCALAR)
+            place(3, slots, dense[3, slots.start][:], SCALAR)

@@ -213,15 +213,18 @@ def tile_attend_gnce_w_kernel(tc, xT, w_words, w_scales, y, wt, xm, offs, out):
             scores(1, t, ALL)
         weigh_y(0, 2, SCALAR)
         weigh_y(0, 0, VECTOR)
+        windows.append(sb("window2", [P, T], F32, tag="y_raw00"))
+        clear_on_gpsimd(windows[2])
         grad(0, 0, ALL)
         grad(0, 1, ALL)
-        weigh_y(0, 3, VECTOR)
+        windows.append(sb("window3", [P, T], F32, tag="xt_codes0"))
+        clear_on_gpsimd(windows[3])
+        nc.vector.tensor_tensor(out=wy[0, 3][:], in0=y_raw[0][1][:, 1, :],
+                                in1=w_rows[:, 0, 3:4].to_broadcast([P, N]), op=ALU.mult)
         sig[1, 1] = sb("sig11", [P, 2, N], F32, tag="y_raw01")
         for t in range(2, PACK):
             scores(1, t, ALL)
         grad(0, 3, ALL)
-        windows.append(sb("window2", [P, T], F32, tag="wy03"))
-        clear_on_gpsimd(windows[2])
         grad(0, 2, ALL)
         subtract_y(1, 0)
         subtract_y(1, 1)
@@ -252,8 +255,6 @@ def tile_attend_gnce_w_kernel(tc, xT, w_words, w_scales, y, wt, xm, offs, out):
         cast_xm(2, 0, PASSES, VECTOR)
         leave(0, SECOND, VECTOR)
         quant_xm(2)
-        windows.append(laid("window3", [P, T], F32, 2048))
-        clear_on_gpsimd(windows[3])
         place(0, SECOND, dense[0, HALF][:], VECTOR)
         for slots in HALVES:
             leave(1, slots, SCALAR)

@@ -24,6 +24,7 @@ DBLOCKS = D // P
 BAND = 16
 QUAD = 32
 RUN = 4
+PAIR = 2
 HALF = N // 2
 FIRST, SECOND, ALL = slice(0, HALF), slice(HALF, N), slice(0, N)
 HALVES = (FIRST, SECOND)
@@ -35,14 +36,10 @@ def tile_attend_gnce_w_kernel(tc, xT, w_words, w_scales, y, wt, xm, offs, out):
     nc = tc.nc
     with ExitStack() as ctx:
         keep = ctx.enter_context(tc.tile_pool(name="keep", bufs=1))
-        shared = ctx.enter_context(tc.tile_pool(name="shared", bufs=1))
         psum = ctx.enter_context(tc.psum_pool(name="psum", bufs=2))
 
         def sb(name, shape, dtype, tag=""):
             return keep.tile(shape, dtype, name=name, tag=tag or name, align_bytes=64)
-
-        def laid(name, shape, dtype, at):
-            return shared.tile(shape, dtype, name=name, tag=name, align_bytes=64, offset=at)
 
         def copy(on_vector, dst, src):
             if on_vector:
@@ -99,13 +96,13 @@ def tile_attend_gnce_w_kernel(tc, xT, w_words, w_scales, y, wt, xm, offs, out):
         xt_scale = [sb("xt_scale%d" % c, [P, KP], U8) for c in range(PASSES)]
         sig = {(c, u): sb("sig%d%d" % (c, u), [P, 2, N], F32) for c, u in ((0, 0), (0, 1), (1, 0))}
         diff = {1: sb("diff1", [P, PACK, N], F32)}
-        g_rows = [sb("g_rows%d" % c, [P, PACK, N], BF16) for c in range(PASSES)]
+        g_rows = {0: sb("g_rows0", [P, PACK, N], BF16)}
         g_packed = [[sb("g_packed0%d" % h, [P, HALF, PACK], BF16) for h in range(2)],
                     [sb("g_packed10", [P, HALF, PACK], BF16)]]
-        g_codes = [sb("g_codes%d" % c, [P, N], U32) for c in range(PASSES)]
+        g_codes = {1: sb("g_codes1", [P, N], U32)}
         g_scale = [sb("g_scale%d" % c, [P, N], U8) for c in range(PASSES)]
-        xm_codes = {k: sb("xm_codes%d" % k, [P, PASSES, P], U32) for k in (0, 2, 3)}
-        xm_scale = [sb("xm_scale%d" % k, [P, PASSES, P], U8) for k in range(DBLOCKS)]
+        xm_codes = {k: sb("xm_codes%d" % k, [P, PASSES, P], U32) for k in (0,)}
+        xm_scale = {k: sb("xm_scale%d" % k, [P, PASSES, P], U8) for k in range(2)}
         wy = {}
         xm_bf = {}
         dense = {}
@@ -148,9 +145,11 @@ def tile_attend_gnce_w_kernel(tc, xT, w_words, w_scales, y, wt, xm, offs, out):
             nc.vector.tensor_tensor(out=diff[c][:, 2 * u:2 * u + 2, :], in0=sig[c, u][:], in1=y_raw[c][u][:],
                                     op=ALU.subtract)
 
-        def weigh_diff(c, h):
-            for t in range(PACK):
-                nc.vector.tensor_scalar_mul(g_rows[c][:, t, HALVES[h]], diff[c][:, t, HALVES[h]], w_rows[:, c, t:t + 1])
+        def weigh_and_pack(c, h):
+            weights = w_rows[:, c, :].unsqueeze(1).unsqueeze(3).to_broadcast([P, HALF // PAIR, PACK, PAIR])
+            nc.vector.tensor_tensor(out=packed(c, h).rearrange("p (q i) t -> p q t i", i=PAIR),
+                                    in0=diff[c][:, :, HALVES[h]].rearrange("p t (q i) -> p q t i", i=PAIR),
+                                    in1=weights, op=ALU.mult)
 
         def pack_g(c, h, on_vector):
             copy(on_vector, packed(c, h).rearrange("p (q i) t -> p q t i", i=RUN),
@@ -213,14 +212,13 @@ def tile_attend_gnce_w_kernel(tc, xT, w_words, w_scales, y, wt, xm, offs, out):
             scores(1, t, ALL)
         weigh_y(0, 2, SCALAR)
         weigh_y(0, 0, VECTOR)
-        windows.append(sb("window2", [P, T], F32, tag="y_raw00"))
-        clear_on_gpsimd(windows[2])
+        weigh_y(0, 3, VECTOR)
         grad(0, 0, ALL)
+        windows.append(sb("window2", [P, T], F32, tag="wy00"))
+        clear_on_gpsimd(windows[2])
         grad(0, 1, ALL)
         windows.append(sb("window3", [P, T], F32, tag="xt_codes0"))
         clear_on_gpsimd(windows[3])
-        nc.vector.tensor_tensor(out=wy[0, 3][:], in0=y_raw[0][1][:, 1, :],
-                                in1=w_rows[:, 0, 3:4].to_broadcast([P, N]), op=ALU.mult)
         sig[1, 1] = sb("sig11", [P, 2, N], F32, tag="y_raw01")
         for t in range(2, PACK):
             scores(1, t, ALL)
@@ -234,38 +232,40 @@ def tile_attend_gnce_w_kernel(tc, xT, w_words, w_scales, y, wt, xm, offs, out):
         xm_bf[1] = sb("xm_bf1", [P, PASSES, P, PACK], BF16, tag="sig01")
         for k in range(2):
             cast_xm(k, 0, PASSES, SCALAR)
-        weigh_diff(1, 0)
+        weigh_and_pack(1, 0)
+        g_codes[0] = sb("g_codes0", [P, N], U32, tag="sig10")
         quant_g(0, 0)
-        pack_g(1, 0, VECTOR)
         quant_xm(0)
         quant_g(1, 0)
         leave(0, FIRST, SCALAR)
         place(0, FIRST, dense[0, 0][:], SCALAR)
-        g_rows_late = sb("g_rows_late", [P, PACK, HALF], BF16, tag="xt_scale0")
-        for t in range(PACK):
-            nc.vector.tensor_scalar_mul(g_rows_late[:, t, :], diff[1][:, t, SECOND], w_rows[:, 1, t:t + 1])
+        g_packed[1].append(sb("g_packed11", [P, HALF, PACK], BF16, tag="xt_scale0"))
+        weigh_and_pack(1, 1)
         quant_g(0, 1)
-        g_packed[1].append(laid("g_packed11", [P, HALF, PACK], BF16, 1024))
-        nc.vector.tensor_copy(out=packed(1, 1).rearrange("p (q i) t -> p q t i", i=RUN),
-                              in_=g_rows_late[:].rearrange("p t (q i) -> p q t i", i=RUN))
-        xm_codes[1] = sb("xm_codes1", [P, PASSES, P], U32, tag="xt_scale0")
+        xm_codes[1] = sb("xm_codes1", [P, PASSES, P], U32, tag="diff1")
         quant_xm(1)
         quant_g(1, 1)
-        xm_bf[2] = laid("xm_bf2", [P, PASSES, P, PACK], BF16, 1024)
-        cast_xm(2, 0, PASSES, VECTOR)
-        leave(0, SECOND, VECTOR)
-        quant_xm(2)
-        place(0, SECOND, dense[0, HALF][:], VECTOR)
+        leave(0, SECOND, SCALAR)
+        place(0, SECOND, dense[0, HALF][:], SCALAR)
+        late_bf = sb("late_bf", [P, PASSES, 2 * P, PACK], BF16, tag="xt_scale0")
+        late_codes = sb("late_codes", [P, PASSES, 2 * P], U32)
+        late_scale = sb("late_scale", [P, PASSES, 2 * P], U8)
+        nc.vector.tensor_copy(out=late_bf[:].rearrange("p c (q i) t -> p c q t i", i=RUN),
+                              in_=xm_raw[1][:].rearrange("p c t (q i) -> p c q t i", i=RUN))
+        leave(1, FIRST, VECTOR)
+        nc.vector.quantize_mx(out=late_codes[:].rearrange("p c m -> p (c m)").bitcast(E4M3),
+                              scales=late_scale[:].rearrange("p c m -> p (c m)"),
+                              in_=late_bf[:].rearrange("p c m t -> p (c m t)"))
+        for k in (2, 3):
+            xm_codes[k] = late_codes[:, :, (k - 2) * P:(k - 1) * P]
+            xm_scale[k] = late_scale[:, :, (k - 2) * P:(k - 1) * P]
+        place(1, FIRST, dense[1, 0][:], VECTOR)
+        leave(1, SECOND, SCALAR)
+        place(1, SECOND, dense[1, HALF][:], VECTOR)
         for slots in HALVES:
-            leave(1, slots, SCALAR)
-            place(1, slots, dense[1, slots.start][:], SCALAR)
-        xm_bf[3] = laid("xm_bf3", [P, PASSES, P, PACK], BF16, 0)
-        cast_xm(3, 0, PASSES, VECTOR)
-        leave(2, FIRST, VECTOR)
-        quant_xm(3)
-        leave(2, SECOND, SCALAR)
-        for slots in HALVES:
-            place(2, slots, dense[2, slots.start][:], VECTOR)
-        for slots in HALVES:
-            leave(3, slots, SCALAR)
-            place(3, slots, dense[3, slots.start][:], SCALAR)
+            leave(2, slots, SCALAR)
+            place(2, slots, dense[2, slots.start][:], SCALAR)
+        leave(3, FIRST, VECTOR)
+        place(3, FIRST, dense[3, 0][:], VECTOR)
+        leave(3, SECOND, SCALAR)
+        place(3, SECOND, dense[3, HALF][:], VECTOR)

@@ -53,7 +53,8 @@ def tile_attend_gnce_w_kernel(tc, xT, w_words, w_scales, y, wt, xm, offs, out):
         offsets = keep.tile([P, N // BAND], U16, name="offsets")
         xt_raw = {(c, 0): sb("xt_raw%d" % c, [P, PACK, KP], F32) for c in range(PASSES)}
         y_raw = [[sb("y_raw%d%d" % (c, u), [P, 2, N], F32) for u in range(2)] for c in range(PASSES)]
-        xm_raw = [sb("xm_raw%d" % h, [P, PASSES, PACK, D // 2], F32) for h in range(2)]
+        xm_parts = ((0, 1), (1, 2), (2, 4))
+        xm_raw = {k0: sb("xm_raw%d" % k0, [P, PASSES, PACK, (k1 - k0) * P], F32) for k0, k1 in xm_parts}
         words = sb("words", [P, T], U32)
         scales = sb("scales", [P, T], U8)
         w_rows = sb("w_rows", [P, PASSES, PACK], F32)
@@ -66,9 +67,9 @@ def tile_attend_gnce_w_kernel(tc, xT, w_words, w_scales, y, wt, xm, offs, out):
             y_rows = y[0][c * KP:(c + 1) * KP, :].rearrange("(p t) i -> p t i", t=PACK)
             nc.sync.dma_start(out=y_raw[c][u][:], in_=y_rows[:, 2 * u:2 * u + 2, :])
 
-        def load_xm(c, h):
-            rows = xm[0][c * KP:(c + 1) * KP, h * (D // 2):(h + 1) * (D // 2)]
-            nc.sync.dma_start(out=xm_raw[h][:, c], in_=rows.rearrange("(p t) d -> p t d", t=PACK))
+        def load_xm(c, k0, k1):
+            rows = xm[0][c * KP:(c + 1) * KP, k0 * P:k1 * P]
+            nc.sync.dma_start(out=xm_raw[k0][:, c], in_=rows.rearrange("(p t) d -> p t d", t=PACK))
 
         load_xt(0, 0, P)
         nc.sync.dma_start(offsets[:], offs)
@@ -81,9 +82,9 @@ def tile_attend_gnce_w_kernel(tc, xT, w_words, w_scales, y, wt, xm, offs, out):
         for c in range(PASSES):
             for u in range(2):
                 load_y(c, u)
-        for h in range(2):
+        for k0, k1 in xm_parts:
             for c in range(PASSES):
-                load_xm(c, h)
+                load_xm(c, k0, k1)
 
         windows = [sb("window%d" % k, [P, T], F32) for k in range(2)]
         for window in windows:
@@ -97,8 +98,7 @@ def tile_attend_gnce_w_kernel(tc, xT, w_words, w_scales, y, wt, xm, offs, out):
         sig = {(c, u): sb("sig%d%d" % (c, u), [P, 2, N], F32) for c, u in ((0, 0), (0, 1), (1, 0))}
         diff = {1: sb("diff1", [P, PACK, N], F32)}
         g_rows = {0: sb("g_rows0", [P, PACK, N], BF16)}
-        g_packed = [[sb("g_packed0%d" % h, [P, HALF, PACK], BF16) for h in range(2)],
-                    [sb("g_packed10", [P, HALF, PACK], BF16)]]
+        g_packed = [[sb("g_packed%d0" % c, [P, HALF, PACK], BF16)] for c in range(PASSES)]
         g_codes = {1: sb("g_codes1", [P, N], U32)}
         g_scale = [sb("g_scale%d" % c, [P, N], U8) for c in range(PASSES)]
         xm_codes = {k: sb("xm_codes%d" % k, [P, PASSES, P], U32) for k in (0,)}
@@ -160,9 +160,8 @@ def tile_attend_gnce_w_kernel(tc, xT, w_words, w_scales, y, wt, xm, offs, out):
                                   in_=packed(c, h).rearrange("p i t -> p (i t)"))
 
         def cast_xm(k, c0, c1, on_vector):
-            cols = slice((k % 2) * P, (k % 2 + 1) * P)
             copy(on_vector, xm_bf[k][:, c0:c1].rearrange("p c (q i) t -> p c q t i", i=RUN),
-                 xm_raw[k // 2][:, c0:c1, :, cols].rearrange("p c t (q i) -> p c q t i", i=RUN))
+                 xm_raw[k][:, c0:c1].rearrange("p c t (q i) -> p c q t i", i=RUN))
 
         def quant_xm(k):
             nc.vector.quantize_mx(out=xm_codes[k][:].rearrange("p c m -> p (c m)").bitcast(E4M3),
@@ -227,11 +226,12 @@ def tile_attend_gnce_w_kernel(tc, xT, w_words, w_scales, y, wt, xm, offs, out):
         subtract_y(1, 0)
         subtract_y(1, 1)
         pack_g(0, 0, SCALAR)
-        pack_g(0, 1, SCALAR)
         xm_bf[0] = sb("xm_bf0", [P, PASSES, P, PACK], BF16, tag="xt_scale0")
+        cast_xm(0, 0, PASSES, SCALAR)
+        g_packed[0].append(sb("g_packed01", [P, HALF, PACK], BF16, tag="xm_raw0"))
+        pack_g(0, 1, SCALAR)
         xm_bf[1] = sb("xm_bf1", [P, PASSES, P, PACK], BF16, tag="sig01")
-        for k in range(2):
-            cast_xm(k, 0, PASSES, SCALAR)
+        cast_xm(1, 0, PASSES, SCALAR)
         weigh_and_pack(1, 0)
         g_codes[0] = sb("g_codes0", [P, N], U32, tag="sig10")
         quant_g(0, 0)
@@ -242,16 +242,16 @@ def tile_attend_gnce_w_kernel(tc, xT, w_words, w_scales, y, wt, xm, offs, out):
         g_packed[1].append(sb("g_packed11", [P, HALF, PACK], BF16, tag="xt_scale0"))
         weigh_and_pack(1, 1)
         quant_g(0, 1)
-        xm_codes[1] = sb("xm_codes1", [P, PASSES, P], U32, tag="diff1")
-        quant_xm(1)
         quant_g(1, 1)
+        xm_codes[1] = sb("xm_codes1", [P, PASSES, P], U32, tag="g_packed10")
+        quant_xm(1)
         leave(0, SECOND, SCALAR)
         place(0, SECOND, dense[0, HALF][:], SCALAR)
         late_bf = sb("late_bf", [P, PASSES, 2 * P, PACK], BF16, tag="xt_scale0")
         late_codes = sb("late_codes", [P, PASSES, 2 * P], U32)
         late_scale = sb("late_scale", [P, PASSES, 2 * P], U8)
         nc.vector.tensor_copy(out=late_bf[:].rearrange("p c (q i) t -> p c q t i", i=RUN),
-                              in_=xm_raw[1][:].rearrange("p c t (q i) -> p c q t i", i=RUN))
+                              in_=xm_raw[2][:].rearrange("p c t (q i) -> p c q t i", i=RUN))
         leave(1, FIRST, VECTOR)
         nc.vector.quantize_mx(out=late_codes[:].rearrange("p c m -> p (c m)").bitcast(E4M3),
                               scales=late_scale[:].rearrange("p c m -> p (c m)"),

@@ -1,6 +1,7 @@
 from contextlib import ExitStack
 
 import concourse.mybir as mybir
+from concourse.masks import make_identity
 
 N, T, D, R = 512, 2048, 512, 1024
 FLOPS = 2 * 2 * R * N * D
@@ -57,6 +58,7 @@ def tile_attend_gnce_w_kernel(tc, xT, w_words, w_scales, y, wt, xm, offs, out):
         xm_raw = {k0: sb("xm_raw%d" % k0, [P, PASSES, PACK, (k1 - k0) * P], F32) for k0, k1 in xm_parts}
         words = sb("words", [P, T], U32)
         scales = sb("scales", [P, T], U8)
+        w_line = sb("w_line", [P, KP], F32)
         w_rows = sb("w_rows", [P, PASSES, PACK], F32)
 
         def load_xt(c, m0, m1):
@@ -76,7 +78,8 @@ def tile_attend_gnce_w_kernel(tc, xT, w_words, w_scales, y, wt, xm, offs, out):
         nc.vector.memset(scales[:].bitcast(I32), 0)
         for f in range(4):
             nc.sync.dma_start(out=scales[f:P:QUAD, :].bitcast(I32), in_=w_scales[0][f:16:4, :].bitcast(I32))
-        nc.scalar.dma_start(out=w_rows[:], in_=wt[0].rearrange("(c p t) o -> p c (t o)", p=P, t=PACK))
+        nc.gpsimd.memset(w_line[:], 0.0)
+        nc.scalar.dma_start(out=w_line[:PASSES, :], in_=wt[0].rearrange("(c r) o -> c (r o)", c=PASSES))
         nc.sync.dma_start(out=words[:].bitcast(I32), in_=w_words[0].rearrange("p n t -> p (n t)").bitcast(I32))
         load_xt(1, 0, P)
         for c in range(PASSES):
@@ -89,6 +92,13 @@ def tile_attend_gnce_w_kernel(tc, xT, w_words, w_scales, y, wt, xm, offs, out):
         windows = [sb("window%d" % k, [P, T], F32) for k in range(2)]
         for window in windows:
             nc.vector.memset(window[:].bitcast(I32), 0)
+
+        identity = sb("identity", [P, P], F32)
+        make_identity(nc, identity[:])
+        w_turned = psum.tile([P, PACK, P], F32, name="w_turned", tag="acc_d", bufs=4)
+        for t in range(PACK):
+            nc.tensor.transpose(w_turned[:, t, :], w_line[:, t:KP:PACK], identity[:])
+        nc.scalar.copy(out=w_rows[:], in_=w_turned[:, :, :PASSES].rearrange("p t c -> p c t"))
 
         w_scale_g = sb("w_scale_g", [P, N], U8)
         w_word_g = sb("w_word_g", [P, N], U32)

@@ -82,12 +82,13 @@ def tile_attend_gnce_w_kernel(tc, xT, w_words, w_scales, y, wt, xm, offs, out):
         nc.scalar.dma_start(out=w_line[:PASSES, :], in_=wt[0].rearrange("(c r) o -> c (r o)", c=PASSES))
         nc.sync.dma_start(out=words[:].bitcast(I32), in_=w_words[0].rearrange("p n t -> p (n t)").bitcast(I32))
         load_xt(1, 0, P)
-        for c in range(PASSES):
-            for u in range(2):
-                load_y(c, u)
+        for c, u in ((0, 0), (0, 1), (1, 0)):
+            load_y(c, u)
         for k0, k1 in xm_parts:
             for c in range(PASSES):
                 load_xm(c, k0, k1)
+            if k0 == 0:
+                load_y(1, 1)
 
         windows = [sb("window%d" % k, [P, T], F32) for k in range(2)]
         for window in windows:

@@ -90,7 +90,7 @@ def tile_attend_gnce_w_kernel(tc, xT, w_words, w_scales, y, wt, xm, offs, out):
             if k0 == 0:
                 load_y(1, 1)
 
-        windows = [sb("window%d" % k, [P, T], F32) for k in range(2)]
+        windows = [sb("window%d" % k, [P, T], F32) for k in range(3)]
         for window in windows:
             nc.vector.memset(window[:].bitcast(I32), 0)
 
@@ -224,11 +224,9 @@ def tile_attend_gnce_w_kernel(tc, xT, w_words, w_scales, y, wt, xm, offs, out):
         weigh_y(0, 0, VECTOR)
         weigh_y(0, 3, VECTOR)
         grad(0, 0, ALL)
-        windows.append(sb("window2", [P, T], F32, tag="wy00"))
-        clear_on_gpsimd(windows[2])
-        grad(0, 1, ALL)
-        windows.append(sb("window3", [P, T], F32, tag="xt_codes0"))
+        windows.append(sb("window3", [P, T], F32, tag="wy00"))
         clear_on_gpsimd(windows[3])
+        grad(0, 1, ALL)
         sig[1, 1] = sb("sig11", [P, 2, N], F32, tag="y_raw01")
         for t in range(2, PACK):
             scores(1, t, ALL)

@@ -40,7 +40,7 @@ def tile_attend_gnce_w_kernel(tc, xT, w_words, w_scales, y, wt, xm, offs, out):
         psum = ctx.enter_context(tc.psum_pool(name="psum", bufs=2))
 
         def sb(name, shape, dtype, tag=""):
-            return keep.tile(shape, dtype, name=name, tag=tag or name, align_bytes=64)
+            return keep.tile(shape, dtype, name=name, tag=tag or name, align_bytes=256)
 
         def copy(on_vector, dst, src):
             if on_vector:

@@ -29,7 +29,7 @@ PAIR = 2
 HALF = N // 2
 FIRST, SECOND, ALL = slice(0, HALF), slice(HALF, N), slice(0, N)
 HALVES = (FIRST, SECOND)
-XT0_VECTOR = 32
+XT0_VECTOR = 40
 VECTOR, SCALAR = True, False
 
 
@@ -103,9 +103,8 @@ def tile_attend_gnce_w_kernel(tc, xT, w_words, w_scales, y, wt, xm, offs, out):
 
         w_scale_g = sb("w_scale_g", [P, N], U8)
         w_word_g = sb("w_word_g", [P, N], U32)
-        xt_bf = [sb("xt_bf%d" % c, [P, PACK, P, PACK], BF16) for c in range(PASSES)]
-        xt_codes = [sb("xt_codes%d" % c, [P, KP], U32) for c in range(PASSES)]
-        xt_scale = [sb("xt_scale%d" % c, [P, KP], U8) for c in range(PASSES)]
+        xt_bf = {0: sb("xt_bf", [P, PACK, P, PACK], BF16)}
+        xt_codes, xt_scale = {}, {}
         sig = {(c, u): sb("sig%d%d" % (c, u), [P, 2, N], F32) for c, u in ((0, 0), (0, 1), (1, 0))}
         diff = {1: sb("diff1", [P, PACK, N], F32)}
         g_rows = {0: sb("g_rows0", [P, PACK, N], BF16)}
@@ -129,14 +128,18 @@ def tile_attend_gnce_w_kernel(tc, xT, w_words, w_scales, y, wt, xm, offs, out):
             copy(on_vector, xt_bf[c][:].rearrange("p t m j -> p m j t")[:, m0:m1],
                  xt_raw[c, part][:].rearrange("p j (m t) -> p m j t", t=PACK)[:, m0 - part:m1 - part])
 
-        def quant_xt(c, t0, t1):
-            nc.vector.quantize_mx(out=xt_codes[c][:, t0 * P:t1 * P].bitcast(E4M3), scales=xt_scale[c][:, t0 * P:t1 * P],
+        def quant_xt(c, t0, t1, tag=""):
+            codes = sb("xt_codes%d%d" % (c, t0), [P, (t1 - t0) * P], U32, tag=tag)
+            scale = sb("xt_scale%d%d" % (c, t0), [P, (t1 - t0) * P], U8)
+            nc.vector.quantize_mx(out=codes[:].bitcast(E4M3), scales=scale[:],
                                   in_=xt_bf[c][:, t0:t1].rearrange("p t m j -> p (t m j)"))
+            for t in range(t0, t1):
+                xt_codes[c, t] = codes[:, (t - t0) * P:(t - t0 + 1) * P]
+                xt_scale[c, t] = scale[:, (t - t0) * P:(t - t0 + 1) * P]
 
         def scores(c, t, slots):
             acc = psum.tile([P, slots.stop - slots.start], F32, name="acc_a", tag="acc_a", bufs=4)
-            cols = slice(t * P, (t + 1) * P)
-            nc.tensor.matmul_mx(out=acc[:], lhsT=xt_codes[c][:, cols].bitcast(E4M3), lhsT_scale=xt_scale[c][:, cols],
+            nc.tensor.matmul_mx(out=acc[:], lhsT=xt_codes[c, t].bitcast(E4M3), lhsT_scale=xt_scale[c, t],
                                 rhs=w_word_g[:, slots].bitcast(E4M3), rhs_scale=w_scale_g[:, slots], start=True, stop=True)
             nc.scalar.activation(out=sig[c, t // 2][:, t % 2, slots], in_=acc[:], func=ACT.Sigmoid)
 
@@ -201,21 +204,23 @@ def tile_attend_gnce_w_kernel(tc, xT, w_words, w_scales, y, wt, xm, offs, out):
                 nc.sync.dma_start(out=out[k * P:(k + 1) * P, :], in_=windows[k][:])
 
         cast_xt(0, 0, XT0_VECTOR, P, SCALAR)
-        nc.vector.tensor_copy(w_scale_g[:], scales[:].indirect(entries(ALL)))
         cast_xt(0, 0, 0, XT0_VECTOR, VECTOR)
-        quant_xt(0, 0, 4)
+        nc.vector.tensor_copy(w_scale_g[:], scales[:].indirect(entries(ALL)))
+        quant_xt(0, 0, 2)
         for slots in HALVES:
             nc.vector.tensor_copy(w_word_g[:, slots], words[:].indirect(entries(slots)))
+        quant_xt(0, 2, 4, tag="words")
         for slots in HALVES:
             for t in range(2):
                 scores(0, t, slots)
         for t in range(2, PACK):
             scores(0, t, ALL)
+        xt_bf[1] = sb("xt_bf1", [P, PACK, P, PACK], BF16, tag="xt_bf")
         cast_xt(1, 0, 0, P, VECTOR)
         quant_xt(1, 0, 4)
         wy[0, 0] = sb("wy00", [P, N], F32)
-        wy[0, 1] = sb("wy01", [P, N], F32, tag="xt_codes0")
-        wy[0, 2] = sb("wy02", [P, N], F32, tag="xt_scale0")
+        wy[0, 1] = sb("wy01", [P, N], F32, tag="words")
+        wy[0, 2] = sb("wy02", [P, N], F32, tag="xt_scale02")
         wy[0, 3] = sb("wy03", [P, N], F32)
         weigh_y(0, 1, SCALAR)
         for t in range(2):
@@ -235,7 +240,7 @@ def tile_attend_gnce_w_kernel(tc, xT, w_words, w_scales, y, wt, xm, offs, out):
         subtract_y(1, 0)
         subtract_y(1, 1)
         pack_g(0, 0, SCALAR)
-        xm_bf[0] = sb("xm_bf0", [P, PASSES, P, PACK], BF16, tag="xt_scale0")
+        xm_bf[0] = sb("xm_bf0", [P, PASSES, P, PACK], BF16, tag="xt_scale02")
         cast_xm(0, 0, PASSES, SCALAR)
         g_packed[0].append(sb("g_packed01", [P, HALF, PACK], BF16, tag="xm_raw0"))
         pack_g(0, 1, SCALAR)
@@ -248,7 +253,7 @@ def tile_attend_gnce_w_kernel(tc, xT, w_words, w_scales, y, wt, xm, offs, out):
         quant_g(1, 0)
         leave(0, FIRST, SCALAR)
         place(0, FIRST, dense[0, 0][:], SCALAR)
-        g_packed[1].append(sb("g_packed11", [P, HALF, PACK], BF16, tag="xt_scale0"))
+        g_packed[1].append(sb("g_packed11", [P, HALF, PACK], BF16, tag="xt_scale02"))
         weigh_and_pack(1, 1)
         quant_g(0, 1)
         quant_g(1, 1)
@@ -256,7 +261,7 @@ def tile_attend_gnce_w_kernel(tc, xT, w_words, w_scales, y, wt, xm, offs, out):
         quant_xm(1)
         leave(0, SECOND, SCALAR)
         place(0, SECOND, dense[0, HALF][:], SCALAR)
-        late_bf = sb("late_bf", [P, PASSES, 2 * P, PACK], BF16, tag="xt_scale0")
+        late_bf = sb("late_bf", [P, PASSES, 2 * P, PACK], BF16, tag="xt_scale02")
         late_codes = sb("late_codes", [P, PASSES, 2 * P], U32)
         late_scale = sb("late_scale", [P, PASSES, 2 * P], U8)
         nc.vector.tensor_copy(out=late_bf[:].rearrange("p c (q i) t -> p c q t i", i=RUN),

from contextlib import ExitStack

import concourse.mybir as mybir
from concourse.masks import make_identity

N, T, D, R = 512, 2048, 512, 1024
FLOPS = 2 * 2 * R * N * D

F32 = mybir.dt.float32
BF16 = mybir.dt.bfloat16
I32 = mybir.dt.int32
U32 = mybir.dt.uint32
U16 = mybir.dt.uint16
U8 = mybir.dt.uint8
E4M3 = mybir.dt.float8_e4m3fn_x4
E5M2 = mybir.dt.float8_e5m2_x4
ACT = mybir.ActivationFunctionType
ALU = mybir.AluOpType

P = 128
PACK = 4
KP = P * PACK
PASSES = R // KP
DBLOCKS = D // P
BAND = 16
QUAD = 32
RUN = 4
PAIR = 2
HALF = N // 2
FIRST, SECOND, ALL = slice(0, HALF), slice(HALF, N), slice(0, N)
HALVES = (FIRST, SECOND)
XT0_VECTOR = 40
VECTOR, SCALAR = True, False


def tile_attend_gnce_w_kernel(tc, xT, w_words, w_scales, y, wt, xm, offs, out):
    nc = tc.nc
    with ExitStack() as ctx:
        keep = ctx.enter_context(tc.tile_pool(name="keep", bufs=1))
        psum = ctx.enter_context(tc.psum_pool(name="psum", bufs=2))

        def sb(name, shape, dtype, tag=""):
            return keep.tile(shape, dtype, name=name, tag=tag or name, align_bytes=256)

        def copy(on_vector, dst, src):
            if on_vector:
                nc.vector.tensor_copy(out=dst, in_=src)
            else:
                nc.scalar.copy(out=dst, in_=src)

        def entries(slots):
            return offsets[:, slots.start // BAND:slots.stop // BAND]

        offsets = keep.tile([P, N // BAND], U16, name="offsets")
        xt_raw = {(c, 0): sb("xt_raw%d" % c, [P, PACK, KP], F32) for c in range(PASSES)}
        y_raw = [[sb("y_raw%d%d" % (c, u), [P, 2, N], F32) for u in range(2)] for c in range(PASSES)]
        xm_parts = ((0, 1), (1, 2), (2, 4))
        xm_raw = {k0: sb("xm_raw%d" % k0, [P, PASSES, PACK, (k1 - k0) * P], F32) for k0, k1 in xm_parts}
        words = sb("words", [P, T], U32)
        scales = sb("scales", [P, T], U8)
        w_line = sb("w_line", [P, KP], F32)
        w_rows = sb("w_rows", [P, PASSES, PACK], F32)

        def load_xt(c, m0, m1):
            rows = xT[0][:, c * KP + PACK * m0:c * KP + PACK * m1]
            nc.sync.dma_start(out=xt_raw[c, m0][:], in_=rows.rearrange("(p j) r -> p j r", j=PACK))

        def load_y(c, u):
            y_rows = y[0][c * KP:(c + 1) * KP, :].rearrange("(p t) i -> p t i", t=PACK)
            nc.sync.dma_start(out=y_raw[c][u][:], in_=y_rows[:, 2 * u:2 * u + 2, :])

        def load_xm(c, k0, k1):
            rows = xm[0][c * KP:(c + 1) * KP, k0 * P:k1 * P]
            nc.sync.dma_start(out=xm_raw[k0][:, c], in_=rows.rearrange("(p t) d -> p t d", t=PACK))

        load_xt(0, 0, P)
        nc.sync.dma_start(offsets[:], offs)
        nc.vector.memset(scales[:].bitcast(I32), 0)
        for f in range(4):
            nc.sync.dma_start(out=scales[f:P:QUAD, :].bitcast(I32), in_=w_scales[0][f:16:4, :].bitcast(I32))
        nc.gpsimd.memset(w_line[:], 0.0)
        nc.scalar.dma_start(out=w_line[:PASSES, :], in_=wt[0].rearrange("(c r) o -> c (r o)", c=PASSES))
        nc.sync.dma_start(out=words[:].bitcast(I32), in_=w_words[0].rearrange("p n t -> p (n t)").bitcast(I32))
        load_xt(1, 0, P)
        for c, u in ((0, 0), (0, 1), (1, 0)):
            load_y(c, u)
        for k0, k1 in xm_parts:
            for c in range(PASSES):
                load_xm(c, k0, k1)
            if k0 == 0:
                load_y(1, 1)

        windows = [sb("window%d" % k, [P, T], F32) for k in range(3)]
        for window in windows:
            nc.vector.memset(window[:].bitcast(I32), 0)

        identity = sb("identity", [P, P], F32)
        make_identity(nc, identity[:])
        w_turned = psum.tile([P, PACK, P], F32, name="w_turned", tag="acc_d", bufs=4)
        for t in range(PACK):
            nc.tensor.transpose(w_turned[:, t, :], w_line[:, t:KP:PACK], identity[:])
        nc.scalar.copy(out=w_rows[:], in_=w_turned[:, :, :PASSES].rearrange("p t c -> p c t"))

        w_scale_g = sb("w_scale_g", [P, N], U8)
        w_word_g = sb("w_word_g", [P, N], U32)
        xt_bf = {0: sb("xt_bf", [P, PACK, P, PACK], BF16)}
        xt_codes, xt_scale = {}, {}
        sig = {(c, u): sb("sig%d%d" % (c, u), [P, 2, N], F32) for c, u in ((0, 0), (0, 1), (1, 0))}
        diff = {1: sb("diff1", [P, PACK, N], F32)}
        g_rows = {0: sb("g_rows0", [P, PACK, N], BF16)}
        g_packed = [[sb("g_packed%d0" % c, [P, HALF, PACK], BF16)] for c in range(PASSES)]
        g_codes = {1: sb("g_codes1", [P, N], U32)}
        g_scale = [sb("g_scale%d" % c, [P, N], U8) for c in range(PASSES)]
        xm_codes = {k: sb("xm_codes%d" % k, [P, PASSES, P], U32) for k in (0,)}
        xm_scale = {k: sb("xm_scale%d" % k, [P, PASSES, P], U8) for k in range(2)}
        wy = {}
        xm_bf = {}
        dense = {}

        def packed(c, h):
            return g_packed[c][h][:]

        def clear_on_gpsimd(window):
            for part in range(2):
                nc.gpsimd.memset(window[:, part * T // 2:(part + 1) * T // 2].bitcast(I32), 0)

        def cast_xt(c, part, m0, m1, on_vector):
            copy(on_vector, xt_bf[c][:].rearrange("p t m j -> p m j t")[:, m0:m1],
                 xt_raw[c, part][:].rearrange("p j (m t) -> p m j t", t=PACK)[:, m0 - part:m1 - part])

        def quant_xt(c, t0, t1, tag=""):
            codes = sb("xt_codes%d%d" % (c, t0), [P, (t1 - t0) * P], U32, tag=tag)
            scale = sb("xt_scale%d%d" % (c, t0), [P, (t1 - t0) * P], U8)
            nc.vector.quantize_mx(out=codes[:].bitcast(E4M3), scales=scale[:],
                                  in_=xt_bf[c][:, t0:t1].rearrange("p t m j -> p (t m j)"))
            for t in range(t0, t1):
                xt_codes[c, t] = codes[:, (t - t0) * P:(t - t0 + 1) * P]
                xt_scale[c, t] = scale[:, (t - t0) * P:(t - t0 + 1) * P]

        def scores(c, t, slots):
            acc = psum.tile([P, slots.stop - slots.start], F32, name="acc_a", tag="acc_a", bufs=4)
            nc.tensor.matmul_mx(out=acc[:], lhsT=xt_codes[c, t].bitcast(E4M3), lhsT_scale=xt_scale[c, t],
                                rhs=w_word_g[:, slots].bitcast(E4M3), rhs_scale=w_scale_g[:, slots], start=True, stop=True)
            nc.scalar.activation(out=sig[c, t // 2][:, t % 2, slots], in_=acc[:], func=ACT.Sigmoid)

        def weigh_y(c, t, on_vector):
            dst = wy[c, t][:]
            if on_vector:
                nc.vector.tensor_scalar_mul(dst, y_raw[c][t // 2][:, t % 2, :], w_rows[:, c, t:t + 1])
            else:
                nc.scalar.activation(out=dst, in_=y_raw[c][t // 2][:, t % 2, :], func=ACT.Copy, scale=w_rows[:, c, t:t + 1])

        def grad(c, t, slots):
            nc.vector.scalar_tensor_tensor(out=g_rows[c][:, t, slots], in0=sig[c, t // 2][:, t % 2, slots],
                                           scalar=w_rows[:, c, t:t + 1], in1=wy[c, t][:, slots],
                                           op0=ALU.mult, op1=ALU.subtract)

        def subtract_y(c, u):
            nc.vector.tensor_tensor(out=diff[c][:, 2 * u:2 * u + 2, :], in0=sig[c, u][:], in1=y_raw[c][u][:],
                                    op=ALU.subtract)

        def weigh_and_pack(c, h):
            weights = w_rows[:, c, :].unsqueeze(1).unsqueeze(3).to_broadcast([P, HALF // PAIR, PACK, PAIR])
            nc.vector.tensor_tensor(out=packed(c, h).rearrange("p (q i) t -> p q t i", i=PAIR),
                                    in0=diff[c][:, :, HALVES[h]].rearrange("p t (q i) -> p q t i", i=PAIR),
                                    in1=weights, op=ALU.mult)

        def pack_g(c, h, on_vector):
            copy(on_vector, packed(c, h).rearrange("p (q i) t -> p q t i", i=RUN),
                 g_rows[c][:, :, HALVES[h]].rearrange("p t (q i) -> p q t i", i=RUN))

        def quant_g(c, h):
            nc.vector.quantize_mx(out=g_codes[c][:, HALVES[h]].bitcast(E5M2), scales=g_scale[c][:, HALVES[h]],
                                  in_=packed(c, h).rearrange("p i t -> p (i t)"))

        def cast_xm(k, c0, c1, on_vector):
            copy(on_vector, xm_bf[k][:, c0:c1].rearrange("p c (q i) t -> p c q t i", i=RUN),
                 xm_raw[k][:, c0:c1].rearrange("p c t (q i) -> p c q t i", i=RUN))

        def quant_xm(k):
            nc.vector.quantize_mx(out=xm_codes[k][:].rearrange("p c m -> p (c m)").bitcast(E4M3),
                                  scales=xm_scale[k][:].rearrange("p c m -> p (c m)"),
                                  in_=xm_bf[k][:, :].rearrange("p c m t -> p (c m t)"))

        def product(k, slots):
            acc = psum.tile([P, slots.stop - slots.start], F32, name="acc_d", tag="acc_d", bufs=4)
            for c in range(PASSES):
                nc.tensor.matmul_mx(out=acc[:], lhsT=xm_codes[k][:, c, :].bitcast(E4M3), lhsT_scale=xm_scale[k][:, c, :],
                                    rhs=g_codes[c][:, slots].bitcast(E5M2), rhs_scale=g_scale[c][:, slots],
                                    start=(c == 0), stop=(c == PASSES - 1))
            return acc

        def leave(k, slots, on_vector):
            width = slots.stop - slots.start
            dense[k, slots.start] = sb("dense%d_%d" % (k, slots.start), [P, width], F32)
            copy(on_vector, dense[k, slots.start][:], product(k, slots)[:])

        def place(k, slots, values, on_vector):
            if on_vector:
                nc.vector.tensor_copy(windows[k][:].indirect(entries(slots)), values)
            else:
                nc.scalar.activation(out=windows[k][:].indirect(entries(slots)), in_=values, func=ACT.Copy)
            if slots.stop == N:
                nc.sync.dma_start(out=out[k * P:(k + 1) * P, :], in_=windows[k][:])

        cast_xt(0, 0, XT0_VECTOR, P, SCALAR)
        cast_xt(0, 0, 0, XT0_VECTOR, VECTOR)
        nc.vector.tensor_copy(w_scale_g[:], scales[:].indirect(entries(ALL)))
        quant_xt(0, 0, 2)
        for slots in HALVES:
            nc.vector.tensor_copy(w_word_g[:, slots], words[:].indirect(entries(slots)))
        quant_xt(0, 2, 4, tag="words")
        for slots in HALVES:
            for t in range(2):
                scores(0, t, slots)
        for t in range(2, PACK):
            scores(0, t, ALL)
        xt_bf[1] = sb("xt_bf1", [P, PACK, P, PACK], BF16, tag="xt_bf")
        cast_xt(1, 0, 0, P, VECTOR)
        quant_xt(1, 0, 4)
        wy[0, 0] = sb("wy00", [P, N], F32)
        wy[0, 1] = sb("wy01", [P, N], F32, tag="words")
        wy[0, 2] = sb("wy02", [P, N], F32, tag="xt_scale02")
        wy[0, 3] = sb("wy03", [P, N], F32)
        weigh_y(0, 1, SCALAR)
        for t in range(2):
            scores(1, t, ALL)
        weigh_y(0, 2, SCALAR)
        weigh_y(0, 0, VECTOR)
        weigh_y(0, 3, VECTOR)
        grad(0, 0, ALL)
        windows.append(sb("window3", [P, T], F32, tag="wy00"))
        clear_on_gpsimd(windows[3])
        grad(0, 1, ALL)
        sig[1, 1] = sb("sig11", [P, 2, N], F32, tag="y_raw01")
        for t in range(2, PACK):
            scores(1, t, ALL)
        grad(0, 3, ALL)
        grad(0, 2, ALL)
        subtract_y(1, 0)
        subtract_y(1, 1)
        pack_g(0, 0, SCALAR)
        xm_bf[0] = sb("xm_bf0", [P, PASSES, P, PACK], BF16, tag="xt_scale02")
        cast_xm(0, 0, PASSES, SCALAR)
        g_packed[0].append(sb("g_packed01", [P, HALF, PACK], BF16, tag="xm_raw0"))
        pack_g(0, 1, SCALAR)
        xm_bf[1] = sb("xm_bf1", [P, PASSES, P, PACK], BF16, tag="sig01")
        cast_xm(1, 0, PASSES, SCALAR)
        weigh_and_pack(1, 0)
        g_codes[0] = sb("g_codes0", [P, N], U32, tag="sig10")
        quant_g(0, 0)
        quant_xm(0)
        quant_g(1, 0)
        leave(0, FIRST, SCALAR)
        place(0, FIRST, dense[0, 0][:], SCALAR)
        g_packed[1].append(sb("g_packed11", [P, HALF, PACK], BF16, tag="xt_scale02"))
        weigh_and_pack(1, 1)
        quant_g(0, 1)
        quant_g(1, 1)
        xm_codes[1] = sb("xm_codes1", [P, PASSES, P], U32, tag="g_packed10")
        quant_xm(1)
        leave(0, SECOND, SCALAR)
        place(0, SECOND, dense[0, HALF][:], SCALAR)
        late_bf = sb("late_bf", [P, PASSES, 2 * P, PACK], BF16, tag="xt_scale02")
        late_codes = sb("late_codes", [P, PASSES, 2 * P], U32)
        late_scale = sb("late_scale", [P, PASSES, 2 * P], U8)
        nc.vector.tensor_copy(out=late_bf[:].rearrange("p c (q i) t -> p c q t i", i=RUN),
                              in_=xm_raw[2][:].rearrange("p c t (q i) -> p c q t i", i=RUN))
        leave(1, FIRST, VECTOR)
        nc.vector.quantize_mx(out=late_codes[:].rearrange("p c m -> p (c m)").bitcast(E4M3),
                              scales=late_scale[:].rearrange("p c m -> p (c m)"),
                              in_=late_bf[:].rearrange("p c m t -> p (c m t)"))
        for k in (2, 3):
            xm_codes[k] = late_codes[:, :, (k - 2) * P:(k - 1) * P]
            xm_scale[k] = late_scale[:, :, (k - 2) * P:(k - 1) * P]
        place(1, FIRST, dense[1, 0][:], VECTOR)
        leave(1, SECOND, SCALAR)
        place(1, SECOND, dense[1, HALF][:], VECTOR)
        for slots in HALVES:
            leave(2, slots, SCALAR)
            place(2, slots, dense[2, slots.start][:], SCALAR)
        leave(3, FIRST, VECTOR)
        place(3, FIRST, dense[3, 0][:], VECTOR)
        leave(3, SECOND, SCALAR)
        place(3, SECOND, dense[3, HALF][:], VECTOR)
